import numpy as np
import ml_dtypes


def mxq(x, axis, fmt="e4m3"):
    dtype, down = {"e4m3": (ml_dtypes.float8_e4m3fn, 7), "e5m2": (ml_dtypes.float8_e5m2, 14)}[fmt]
    v = np.moveaxis(np.asarray(x, np.float32).astype(ml_dtypes.bfloat16).astype(np.float64), axis, -1)
    blocks = v.reshape(v.shape[:-1] + (-1, 32))
    amax = np.abs(blocks).max(-1, keepdims=True)
    byte = np.maximum(np.where(amax > 0, np.frexp(amax)[1] - 1 + 127, 0) - down, 1)
    scale = np.exp2(byte - 127.0)
    codes = (blocks / scale).astype(np.float32).astype(dtype).astype(np.float64)
    return np.moveaxis((codes * scale).reshape(v.shape), -1, axis)


WIDE = False


def mx_kscale(k):
    if not WIDE:
        return np.ones(k)
    levels = np.array([10, -10, 5, -5, 0])
    if k % 512:
        return np.exp2(np.random.permutation(np.resize(levels, k // 32))).repeat(32)
    a = np.empty((k // 512, 16))
    for p in range(k // 512):
        a[p, :8] = np.random.permutation(np.resize(levels, 8))
        for g in range(8):
            far = levels[np.abs(levels - a[p, g]) >= 10]
            a[p, g + 8] = far[np.random.randint(len(far))]
    return np.exp2(a.ravel()).repeat(32)


BF16 = ml_dtypes.bfloat16


def bf(x):
    return np.asarray(x, np.float32).astype(BF16)


def f64(x):
    return np.asarray(x).astype(np.float64)


E2M1 = np.array([0.0, 0.5, 1.0, 1.5, 2.0, 3.0, 4.0, 6.0, -0.0, -0.5, -1.0, -1.5, -2.0, -3.0, -4.0, -6.0])


def pack_weight(w, fmt):
    k, n = w.shape
    w = f64(bf(w)).reshape(k // 32, 32, n)
    amax = np.abs(w).max(1)
    if fmt == "e4m3":
        byte = np.frexp(amax)[1] - 1 + 127 - 7
    else:
        mant, ex = np.frexp(amax / 6.0)
        byte = np.where(mant > 0.5, ex, ex - 1) + 127
    byte = np.clip(np.where(amax > 0, byte, 1), 1, 254)
    scaled = (w * np.exp2(127.0 - byte)[:, None, :]).reshape(k, n).astype(np.float32)
    by_word = np.ascontiguousarray(scaled.reshape(k // 512, 128, 4, n).transpose(0, 1, 3, 2))
    if fmt == "e4m3":
        words = by_word.astype(ml_dtypes.float8_e4m3fn).view(np.uint8)
    else:
        c = by_word.astype(ml_dtypes.float4_e2m1fn).view(np.uint8) & 0xF
        words = c[..., 0::2] | (c[..., 1::2] << 4)
    return np.ascontiguousarray(words), np.ascontiguousarray(byte.astype(np.uint8).reshape(k // 512, 16, n))


def unpack_weight(words, scales, fmt):
    g, p, n, _ = words.shape
    if fmt == "e4m3":
        vals = np.ascontiguousarray(words).view(ml_dtypes.float8_e4m3fn).astype(np.float64)
    else:
        nib = np.empty((g, p, n, 4), np.uint8)
        nib[..., 0::2] = words & 0xF
        nib[..., 1::2] = words >> 4
        vals = E2M1[nib]
    vals = vals * np.repeat(np.exp2(scales.astype(np.float64) - 127.0), 8, axis=1)[..., None]
    return vals.transpose(0, 1, 3, 2).reshape(g * 512, n)
def pack4(w):
    words, scales = pack_weight(w, "e2m1")
    return words.reshape(words.shape[0], 128, -1), scales


def unpack4(words, scales):
    return unpack_weight(words.reshape(words.shape[0], 128, -1, 2), scales, "e2m1")


def planes(Y):
    n, m = Y.shape
    b = f64(bf(Y)).reshape(n // 32, 32, m)
    amax = np.abs(b).max(1)
    byte = np.clip(np.where(amax > 0, np.frexp(amax)[1] - 1 + 127 - 7, 1), 1, 254)
    codes = (b * np.exp2(127.0 - byte)[:, None, :]).reshape(n, m).astype(np.float32).astype(ml_dtypes.float8_e4m3fn).view(np.uint8)
    words = codes.reshape(n // 512, 128, 4, m).transpose(0, 1, 3, 2)
    return np.ascontiguousarray(words), np.ascontiguousarray(byte.astype(np.uint8).reshape(n // 512, 16, m))


N, D, M, R, F = 512, 1024, 4, 512, 1024


def setup_inputs():
    s, t = mx_kscale(D), mx_kscale(R)
    x = bf(np.random.standard_normal((N, D)) * s)
    w0_words, w0_scales = pack4(np.random.standard_normal((D, F)) / np.sqrt(D) / s[:, None])
    bases = bf(np.random.standard_normal((M, D, R)) / np.sqrt(D) / s[None, :, None])
    lam = bf(np.random.standard_normal((M, R)) * t[None, :])
    a_words, a_scales = pack4(np.random.standard_normal((R, F)) / np.sqrt(R) / t[:, None])
    gam = bf(np.random.standard_normal((M, F)) * 0.5)
    return {
        "x": x,
        "w0_words": w0_words,
        "w0_scales": w0_scales,
        "bases": bases,
        "lam": lam,
        "a_words": a_words,
        "a_scales": a_scales,
        "gam": gam,
    }


def core(x, w0_words, w0_scales, bases, lam, a_words, a_scales, gam):
    xq = mxq(f64(x), 1, "e4m3")
    h = xq @ mxq(f64(bases), 1, "e4m3")
    hl = h * f64(lam)[:, None, :]
    u = mxq(hl, 2, "e4m3") @ unpack4(a_words, a_scales)
    upd = np.sum(u * f64(gam)[:, None, :], axis=0)
    return (xq @ unpack4(w0_words, w0_scales)) + upd


def reference(x, w0_words, w0_scales, bases, lam, a_words, a_scales, gam):
    R_out = core(x, w0_words, w0_scales, bases, lam, a_words, a_scales, gam)
    words, scales = planes(R_out.T)
    return R_out, words, scales

@@ -1,0 +1,360 @@
+from contextlib import ExitStack
+
+import concourse.mybir as mybir
+from concourse.masks import make_identity
+
+TOK, D, NB, R, F = 512, 1024, 4, 512, 1024
+FLOPS = 2 * TOK * D * R * NB + 2 * TOK * R * F * NB + 2 * TOK * D * F
+
+F32 = mybir.dt.float32
+BF16 = mybir.dt.bfloat16
+U32 = mybir.dt.uint32
+I32 = mybir.dt.int32
+U8 = mybir.dt.uint8
+FP8X4 = mybir.dt.float8_e4m3fn_x4
+FP4X4 = mybir.dt.float4_e2m1fn_x4
+MULT = mybir.AluOpType.mult
+ADD = mybir.AluOpType.add
+COPY = mybir.ActivationFunctionType.Copy
+
+P = 128
+KG = D // 512
+TT = TOK // P
+NJ = F // P
+
+S_U = {(2, j) for j in range(NJ)} | {(1, j) for j in (1, 3, 5, 7)}
+VEC_T = (2, 2, 1, 0)
+G_CAST = ()
+VEC_OUT = ()
+VEC_PL = (3,)
+VEC_BASE = ()
+PH2 = 1
+MANUAL = False
+
+
+def tile_randlorafullrankbasissum_x2_kernel(
+    tc, x, w0_words, w0_scales, bases, lam, a_words, a_scales, gam, out_0, out_1, out_2
+):
+    nc = tc.nc
+    with ExitStack() as ctx:
+        keep = ctx.enter_context(tc.tile_pool(name="keep", bufs=1))
+        work = ctx.enter_context(tc.tile_pool(name="work", bufs=2))
+        psum = ctx.enter_context(tc.psum_pool(name="psum", bufs=1))
+
+        def bank_h(name, shape, dtype=F32):
+            return psum.tile(shape, dtype, name=name, tag="bank_h", bufs=3)
+
+        def bank_u(name, shape, dtype=F32):
+            return psum.tile(shape, dtype, name=name, tag="bank_u", bufs=5)
+
+        x_sb = keep.tile([P, TT, D], BF16, name="x_sb", align_bytes=64)
+        xg = keep.tile([P, KG, TOK, 4], BF16, name="xg", align_bytes=64)
+        xq = keep.tile([P, KG, TOK], U32, name="xq", align_bytes=64)
+        xs = keep.tile([P, KG, TOK], U8, name="xs", align_bytes=64)
+        braw = [keep.tile([P, KG, 4, R], BF16, name="braw%d" % m, align_bytes=64) for m in range(NB)]
+        bq = [keep.tile([P, KG, R], U32, name="bq%d" % m, align_bytes=64) for m in range(NB)]
+        bs = [keep.tile([P, KG, R], U8, name="bs%d" % m, align_bytes=64) for m in range(NB)]
+        w0 = keep.tile([P, KG, 2 * F], U8, name="w0", align_bytes=64)
+        aw = keep.tile([P, 2 * F], U8, name="aw", align_bytes=64)
+        wsc = keep.tile([P, KG + 1, F], U8, name="wsc", align_bytes=64)
+        vec = keep.tile([P, R + P], BF16, name="vec", align_bytes=64)
+        ident = keep.tile([P, P], F32, name="ident", align_bytes=64)
+        ident_b = keep.tile([P, P], BF16, name="ident_b", align_bytes=64)
+        lam_t = keep.tile([P, NB, 1, 4], F32, name="lam_t", align_bytes=64)
+        gam_t = keep.tile([P, NB * NJ], F32, name="gam_t", align_bytes=64)
+        acc = keep.tile([P, NJ, TOK], F32, name="acc", align_bytes=64)
+        o32 = keep.tile([P, TT, F], F32, name="o32", align_bytes=64)
+        o16 = keep.tile([P, TT, F], BF16, name="o16", align_bytes=64)
+        pg = keep.tile([P, 2, TOK, 4], BF16, name="pg", align_bytes=64)
+        pq = keep.tile([P, 2, TOK], U32, name="pq", align_bytes=64)
+        ps = keep.tile([P, 2, TOK], U8, name="ps", align_bytes=64)
+        hl = [keep.tile([P, TOK, 4], BF16, name="hl%d" % m, align_bytes=64) for m in range(NB)]
+        hq = [keep.tile([P, TOK], U32, name="hq%d" % m, align_bytes=64) for m in range(NB)]
+        hs = [keep.tile([P, TOK], U8, name="hs%d" % m, align_bytes=64) for m in range(NB)]
+        part = {}
+        for m, j in sorted(S_U):
+            part[(m, j)] = keep.tile([P, TOK], F32, name="part%d_%d" % (m, j), align_bytes=64)
+
+        nc.vector.memset(vec[:], 0.0)
+        nc.gpsimd.memset(wsc[:].rearrange("p a n -> p (a n)").bitcast(I32), 0)
+        make_identity(nc, ident[:])
+        nc.scalar.copy(out=ident_b[:], in_=ident[:])
+        nc.scalar.dma_start(out=vec[0:NB, 0:R], in_=lam[:, :])
+        nc.scalar.dma_start(out=vec[0 : NB * NJ, R : R + P], in_=gam.rearrange("m (j p) -> (m j) p", p=P))
+
+        def load_x(i):
+            nc.sync.dma_start(out=x_sb[:, i, :], in_=x[P * i : P * (i + 1), :])
+
+        def load_b(m):
+            for g in range(KG):
+                nc.sync.dma_start(
+                    out=braw[m][:, g, :, :],
+                    in_=bases[m, 512 * g : 512 * (g + 1), :].rearrange("(p j) r -> p j r", j=4),
+                )
+
+        load_x(0)
+        load_b(0)
+        load_x(1)
+        load_x(2)
+        load_x(3)
+        load_b(1)
+        for q in range(4):
+            nc.sync.dma_start(
+                out=wsc[32 * q : 32 * q + 4, 0:KG, :].bitcast(I32),
+                in_=w0_scales[:, 4 * q : 4 * q + 4, :].rearrange("g q n -> q g n").bitcast(I32),
+            )
+        for q in range(4):
+            nc.sync.dma_start(
+                out=wsc[32 * q : 32 * q + 4, KG, :].bitcast(I32),
+                in_=a_scales[0, 4 * q : 4 * q + 4, :].bitcast(I32),
+            )
+        nc.sync.dma_start(
+            out=w0[:].bitcast(I32),
+            in_=w0_words.rearrange("g p b -> p g b").bitcast(I32),
+        )
+        nc.sync.dma_start(out=aw[:].bitcast(I32), in_=a_words[0].bitcast(I32))
+        load_b(2)
+        load_b(3)
+
+        grouped = {}
+
+        def interleave(m, g):
+            tile_ = work.tile([P, 4 * R], BF16, name="grouped%d_%d" % (m, g), tag="grouped", bufs=6, align_bytes=64)
+            grouped[(m, g)] = tile_
+            v = VEC_T[m]
+            if isinstance(v, tuple):
+                v = v[g]
+            dst = tile_[:].rearrange("p (t c i j) -> p c t i j", t=4, i=2, j=4)
+            srcv = braw[m][:, g, :, :].rearrange("p j (c i t) -> p c t i j", i=2, t=4)
+            cut = 16 * v
+            if v < 4:
+                nc.scalar.copy(out=dst[:, cut:64], in_=srcv[:, cut:64])
+            if v > 0:
+                nc.vector.tensor_copy(out=dst[:, 0:cut], in_=srcv[:, 0:cut])
+
+        def quant_b(m, g):
+            nc.vector.quantize_mx(out=bq[m][:, g, :].bitcast(FP8X4), scales=bs[m][:, g, :], in_=grouped[(m, g)][:])
+
+        def x_turn(i):
+            words = x_sb[:, i, :].bitcast(F32)
+            bank = bank_u("xt%d" % i, [P, KG, 2, P])
+            for g in range(KG):
+                for u in range(2):
+                    nc.tensor.transpose(bank[:, g, u, :], words[:, 256 * g + u : 256 * (g + 1) : 2], ident[:])
+            dst = xg[:, :, P * i : P * (i + 1), :].rearrange("p g n t -> p g (n t)").bitcast(F32)
+            dst = dst.rearrange("p g (n u) -> p g n u", u=2)
+            nc.scalar.copy(out=dst, in_=bank[:].rearrange("p g u n -> p g n u"))
+
+        def quant_x(i0, i1):
+            for g in range(KG):
+                sl = slice(P * i0, P * i1)
+                nc.vector.quantize_mx(
+                    out=xq[:, g, sl].bitcast(FP8X4),
+                    scales=xs[:, g, sl],
+                    in_=xg[:, g, sl, :].rearrange("p n t -> p (n t)"),
+                )
+
+        def stage1(m, i):
+            bank = bank_h("h%d_%d" % (m, i), [P, 4, P])
+            sl = slice(P * i, P * (i + 1))
+            for t in range(4):
+                cols = slice(P * t, P * (t + 1))
+                for g in range(KG):
+                    nc.tensor.matmul_mx(
+                        out=bank[:, t, :],
+                        lhsT=bq[m][:, g, cols].bitcast(FP8X4),
+                        lhsT_scale=bs[m][:, g, cols],
+                        rhs=xq[:, g, sl].bitcast(FP8X4),
+                        rhs_scale=xs[:, g, sl],
+                        start=(g == 0),
+                        stop=(g == KG - 1),
+                    )
+            nc.vector.tensor_tensor(
+                out=hl[m][:, sl, :],
+                in0=bank[:].rearrange("p t n -> p n t"),
+                in1=lam_t[:, m, :, :].to_broadcast([P, P, 4]),
+                op=MULT,
+            )
+
+        def quant_h(m, half):
+            sl = slice(256 * half, 256 * (half + 1))
+            nc.vector.quantize_mx(
+                out=hq[m][:, sl].bitcast(FP8X4), scales=hs[m][:, sl], in_=hl[m][:, sl, :].rearrange("p n t -> p (n t)")
+            )
+
+        def base(j):
+            bank = bank_u("base%d" % j, [P, TOK])
+            for g in range(KG):
+                nc.tensor.matmul_mx(
+                    out=bank[:],
+                    lhsT=w0[:, g, 256 * j : 256 * (j + 1)].bitcast(FP4X4),
+                    lhsT_scale=wsc[:, g, P * j : P * (j + 1)],
+                    rhs=xq[:, g, :].bitcast(FP8X4),
+                    rhs_scale=xs[:, g, :],
+                    start=(g == 0),
+                    stop=(g == KG - 1),
+                )
+            copy = nc.vector.tensor_copy if j in VEC_BASE else nc.scalar.copy
+            copy(out=acc[:, j, :], in_=bank[:])
+
+        def stage2(m, j):
+            bank = bank_u("u%d_%d" % (m, j), [P, TOK])
+            nc.tensor.matmul_mx(
+                out=bank[:],
+                lhsT=aw[:, 256 * j : 256 * (j + 1)].bitcast(FP4X4),
+                lhsT_scale=wsc[:, KG, P * j : P * (j + 1)],
+                rhs=hq[m][:].bitcast(FP8X4),
+                rhs_scale=hs[m][:],
+                start=True,
+                stop=True,
+            )
+            col = gam_t[:, NJ * m + j : NJ * m + j + 1]
+            if (m, j) in S_U:
+                nc.scalar.activation(out=part[(m, j)][:], in_=bank[:], func=COPY, scale=col)
+            else:
+                nc.vector.scalar_tensor_tensor(
+                    out=acc[:, j, :], in0=bank[:], scalar=col, in1=acc[:, j, :], op0=MULT, op1=ADD
+                )
+
+        def out_bank(j):
+            bank = bank_h("o%d" % j, [P, TT, P])
+            parts = [part[key][:] for key in sorted(part) if key[1] == j] + [acc[:, j, :]]
+            for i in range(TT):
+                for n, piece in enumerate(parts):
+                    nc.tensor.matmul(
+                        bank[:, i, :],
+                        lhsT=piece[:, P * i : P * (i + 1)],
+                        rhs=ident[:],
+                        start=(n == 0),
+                        stop=(n == len(parts) - 1),
+                        is_transpose=True,
+                    )
+            cols = slice(P * j, P * (j + 1))
+            copy = nc.vector.tensor_copy if j in VEC_OUT else nc.scalar.copy
+            copy(out=o32[:, :, cols], in_=bank[:])
+
+        def store(j0, j1):
+            cols = slice(P * j0, P * j1)
+            nc.sync.dma_start(out=out_0[:, cols].rearrange("(i p) f -> p i f", p=P), in_=o32[:, :, cols])
+
+        def round_out(j):
+            h, jj = j // 4, j % 4
+            dst = o16[:].rearrange("p i (h u q e) -> p i h u q e", h=2, u=2, e=2)[:, :, h, :, 32 * jj : 32 * (jj + 1), :]
+            src = o32[:, :, P * j : P * (j + 1)].rearrange("p i (q u e) -> p i u q e", u=2, e=2)
+            if j in G_CAST:
+                nc.gpsimd.tensor_scalar(out=dst, in0=src, scalar1=1.0, scalar2=-0.0, op0=MULT, op1=ADD)
+            else:
+                nc.vector.tensor_copy(out=dst, in_=src)
+
+        def plane_turn(h, ip):
+            bank = bank_h("pt%d_%d" % (h, ip), [P, 2, 2, P])
+            for ii in range(2):
+                words = o16[:, 2 * ip + ii, :].bitcast(F32)
+                for u in range(2):
+                    w = 256 * h + 128 * u
+                    nc.tensor.transpose(bank[:, ii, u, :], words[:, w : w + 128], ident[:])
+            sl = slice(256 * ip, 256 * (ip + 1))
+            dst = pg[:, h, sl, :].rearrange("p n t -> p (n t)").bitcast(F32)
+            dst = dst.rearrange("p (i n u) -> p i n u", i=2, u=2)
+            copy = nc.vector.tensor_copy if 2 * h + ip in VEC_PL else nc.scalar.copy
+            copy(out=dst, in_=bank[:].rearrange("p i u n -> p i n u"))
+
+        def plane_quant(h, ip):
+            sl = slice(256 * ip, 256 * (ip + 1))
+            nc.vector.quantize_mx(
+                out=pq[:, h, sl].bitcast(FP8X4), scales=ps[:, h, sl], in_=pg[:, h, sl, :].rearrange("p n t -> p (n t)")
+            )
+            nc.sync.dma_start(
+                out=out_1[h].rearrange("p n t -> p (n t)").bitcast(I32)[:, sl], in_=pq[:, h, sl].bitcast(I32)
+            )
+
+        def plane_scales(h):
+            for q in range(4):
+                eng = nc.sync if q % 2 == 0 else nc.scalar
+                eng.dma_start(
+                    out=out_2[h, 4 * q : 4 * q + 4, :].bitcast(I32), in_=ps[32 * q : 32 * q + 4, h, :].bitcast(I32)
+                )
+
+        def compute():
+            x_turn(0)
+            vbank = bank_u("vbank", [P, 5, P], BF16)
+            for t in range(4):
+                nc.tensor.transpose(vbank[:, t, :], vec[:, t:R:4], ident_b[:])
+            nc.tensor.transpose(vbank[:, 4, :], vec[:, R : R + P], ident_b[:])
+            interleave(0, 0)
+            quant_x(0, 1)
+            interleave(0, 1)
+            quant_b(0, 0)
+            nc.scalar.copy(
+                out=lam_t[:].rearrange("p m o t -> p m (o t)"), in_=vbank[:, 0:4, 0:NB].rearrange("p t m -> p m t")
+            )
+            nc.scalar.copy(out=gam_t[:], in_=vbank[:, 4, 0 : NB * NJ])
+            x_turn(1)
+            quant_b(0, 1)
+            quant_x(1, 2)
+            x_turn(2)
+            x_turn(3)
+            quant_x(2, 4)
+            for s in range(NB + 1):
+                for i in range(4):
+                    if s < NB:
+                        stage1(s, i)
+                    if s + 1 < NB and i < 2:
+                        interleave(s + 1, i)
+                    if s == 1:
+                        base(i)
+                    if s > 0:
+                        stage2(s - 1, i)
+                    if s < NB and i == 2:
+                        quant_h(s, 0)
+                    if s + 1 < NB and i > 1:
+                        quant_b(s + 1, i - 2)
+                if s < NB:
+                    quant_h(s, 1)
+                if PH2 and s > 1:
+                    for j in range(4, 4 + PH2):
+                        if s == 2:
+                            base(j)
+                        stage2(s - 2, j)
+            for j in range(4 + PH2, 8):
+                base(j)
+            for pair in ((4, 5), (6, 7)):
+                for m in range(NB):
+                    for j in pair:
+                        if j >= 4 + PH2 or m == NB - 1:
+                            stage2(m, j)
+                    if pair[0] == 4:
+                        out_bank(m)
+                        if m in (1, 3):
+                            store(m - 1, m + 1)
+                        round_out(m)
+                    if pair[0] == 6:
+                        if m == 0:
+                            plane_turn(0, 0)
+                            plane_turn(0, 1)
+                        if m == 1:
+                            plane_quant(0, 0)
+                            plane_quant(0, 1)
+                            plane_scales(0)
+                        if m == 2:
+                            out_bank(4)
+                            round_out(4)
+                        if m == 3:
+                            out_bank(5)
+                            store(4, 6)
+                            round_out(5)
+            for j in (6, 7):
+                out_bank(j)
+                store(j, j + 1)
+                round_out(j)
+            plane_turn(1, 0)
+            plane_turn(1, 1)
+            plane_quant(1, 0)
+            plane_quant(1, 1)
+            plane_scales(1)
+
+        if MANUAL:
+            with tc.manual_schedule():
+                compute()
+        else:
+            compute()

@@ -21,15 +21,14 @@ P = 128
 KG = D // 512
 TT = TOK // P
 NJ = F // P
-
-S_U = {(2, j) for j in range(NJ)} | {(1, j) for j in (1, 3, 5, 7)}
-VEC_T = (2, 2, 1, 0)
-G_CAST = ()
-VEC_OUT = ()
-VEC_PL = (3,)
-VEC_BASE = ()
-PH2 = 1
-MANUAL = False
+X_RUNS = ((0, 1), (1, 2), (2, 4))
+V_SHARE = (40,24,8,8)
+V_J = (0, 1, 2, 3, 4)
+S_J = (5, 6, 7)
+HELD = (5, 6, 7)
+BASE_AT = {1: (5,), 2: (6,), 3: (7,)}
+S_LAST = (1,)
+LAG = 3
 
 
 def tile_randlorafullrankbasissum_x2_kernel(
@@ -38,124 +37,136 @@ def tile_randlorafullrankbasissum_x2_kernel(
     nc = tc.nc
     with ExitStack() as ctx:
         keep = ctx.enter_context(tc.tile_pool(name="keep", bufs=1))
-        work = ctx.enter_context(tc.tile_pool(name="work", bufs=2))
         psum = ctx.enter_context(tc.psum_pool(name="psum", bufs=1))
+        ctx.enter_context(tc.manual_schedule())
 
-        def bank_h(name, shape, dtype=F32):
-            return psum.tile(shape, dtype, name=name, tag="bank_h", bufs=3)
+        free_banks = list(range(8))
+        bank_number = {}
 
-        def bank_u(name, shape, dtype=F32):
-            return psum.tile(shape, dtype, name=name, tag="bank_u", bufs=5)
+        def sb(name, shape, dtype):
+            return keep.tile(shape, dtype, name=name, align_bytes=64)
 
-        x_sb = keep.tile([P, TT, D], BF16, name="x_sb", align_bytes=64)
-        xg = keep.tile([P, KG, TOK, 4], BF16, name="xg", align_bytes=64)
-        xq = keep.tile([P, KG, TOK], U32, name="xq", align_bytes=64)
-        xs = keep.tile([P, KG, TOK], U8, name="xs", align_bytes=64)
-        braw = [keep.tile([P, KG, 4, R], BF16, name="braw%d" % m, align_bytes=64) for m in range(NB)]
-        bq = [keep.tile([P, KG, R], U32, name="bq%d" % m, align_bytes=64) for m in range(NB)]
-        bs = [keep.tile([P, KG, R], U8, name="bs%d" % m, align_bytes=64) for m in range(NB)]
-        w0 = keep.tile([P, KG, 2 * F], U8, name="w0", align_bytes=64)
-        aw = keep.tile([P, 2 * F], U8, name="aw", align_bytes=64)
-        wsc = keep.tile([P, KG + 1, F], U8, name="wsc", align_bytes=64)
-        vec = keep.tile([P, R + P], BF16, name="vec", align_bytes=64)
-        ident = keep.tile([P, P], F32, name="ident", align_bytes=64)
-        ident_b = keep.tile([P, P], BF16, name="ident_b", align_bytes=64)
-        lam_t = keep.tile([P, NB, 1, 4], F32, name="lam_t", align_bytes=64)
-        gam_t = keep.tile([P, NB * NJ], F32, name="gam_t", align_bytes=64)
-        acc = keep.tile([P, NJ, TOK], F32, name="acc", align_bytes=64)
-        o32 = keep.tile([P, TT, F], F32, name="o32", align_bytes=64)
-        o16 = keep.tile([P, TT, F], BF16, name="o16", align_bytes=64)
-        pg = keep.tile([P, 2, TOK, 4], BF16, name="pg", align_bytes=64)
-        pq = keep.tile([P, 2, TOK], U32, name="pq", align_bytes=64)
-        ps = keep.tile([P, 2, TOK], U8, name="ps", align_bytes=64)
-        hl = [keep.tile([P, TOK, 4], BF16, name="hl%d" % m, align_bytes=64) for m in range(NB)]
-        hq = [keep.tile([P, TOK], U32, name="hq%d" % m, align_bytes=64) for m in range(NB)]
-        hs = [keep.tile([P, TOK], U8, name="hs%d" % m, align_bytes=64) for m in range(NB)]
-        part = {}
-        for m, j in sorted(S_U):
-            part[(m, j)] = keep.tile([P, TOK], F32, name="part%d_%d" % (m, j), align_bytes=64)
+        def new_bank(name, shape, dtype=F32):
+            number = free_banks.pop(0)
+            bank_number[name] = number
+            return psum.tile(shape, dtype, name=name, tag="bank%d" % number, bufs=1)
 
-        nc.vector.memset(vec[:], 0.0)
-        nc.gpsimd.memset(wsc[:].rearrange("p a n -> p (a n)").bitcast(I32), 0)
-        make_identity(nc, ident[:])
-        nc.scalar.copy(out=ident_b[:], in_=ident[:])
-        nc.scalar.dma_start(out=vec[0:NB, 0:R], in_=lam[:, :])
-        nc.scalar.dma_start(out=vec[0 : NB * NJ, R : R + P], in_=gam.rearrange("m (j p) -> (m j) p", p=P))
+        def release(name):
+            free_banks.append(bank_number.pop(name))
+
+        x_sb = [sb("x_sb%d" % i, [P, D], BF16) for i in range(TT)]
+        xg = [sb("xg%d" % n, [P, KG, P * (i1 - i0), 4], BF16) for n, (i0, i1) in enumerate(X_RUNS)]
+        xq = sb("xq", [P, KG, TOK], U32)
+        xs = sb("xs", [P, KG, TOK], U8)
+        braw = {(m, g): sb("braw%d_%d" % (m, g), [P, 4, R], BF16) for m in range(NB) for g in range(KG)}
+        bgr = [sb("bgr%d" % m, [P, KG, 4 * R], BF16) for m in range(NB)]
+        bq = [sb("bq%d" % m, [P, KG, R], U32) for m in range(NB)]
+        bs = [sb("bs%d" % m, [P, KG, R], U8) for m in range(NB)]
+        w0 = sb("w0", [P, KG, 2 * F], U8)
+        aw = sb("aw", [P, 2 * F], U8)
+        w0s = sb("w0s", [P, KG, F], U8)
+        aws = sb("aws", [P, F], U8)
+        gam_rows = sb("gam_rows", [P, P], BF16)
+        ident = sb("ident", [P, P], F32)
+        ident_b = sb("ident_b", [P, P], BF16)
+        lam_t = sb("lam_t", [P, NB, 1, 4], BF16)
+        gam_t = sb("gam_t", [P, NB * NJ], F32)
+        hl = [sb("hl%d" % m, [P, TOK, 4], BF16) for m in range(NB)]
+        hq = [sb("hq%d" % m, [P, TOK], U32) for m in range(NB)]
+        hs = [sb("hs%d" % m, [P, TOK], U8) for m in range(NB)]
+        o32 = [sb("o32_%d" % jp, [P, TT, 2 * P], F32) for jp in range(NJ // 2)]
+        o16 = [sb("o16_%d" % g, [P, TT, 512], BF16) for g in range(2)]
+        pg = {(g, h): sb("pg%d_%d" % (g, h), [P, 256, 4], BF16) for g in range(2) for h in range(2)}
+        pq = [sb("pq%d" % g, [P, TOK], U32) for g in range(2)]
+        ps = sb("ps", [P, TOK], U8)
+        parts = [[] for j in range(NJ)]
+        out_bank = {}
+        held = {}
 
         def load_x(i):
-            nc.sync.dma_start(out=x_sb[:, i, :], in_=x[P * i : P * (i + 1), :])
+            nc.sync.dma_start(out=x_sb[i][:], in_=x[P * i : P * (i + 1), :])
 
-        def load_b(m):
-            for g in range(KG):
+        def load_b(m, g):
+            nc.sync.dma_start(
+                out=braw[(m, g)][:], in_=bases[m, 512 * g : 512 * (g + 1), :].rearrange("(p j) r -> p j r", j=4)
+            )
+
+        def load_w0_scales():
+            for q in range(4):
                 nc.sync.dma_start(
-                    out=braw[m][:, g, :, :],
-                    in_=bases[m, 512 * g : 512 * (g + 1), :].rearrange("(p j) r -> p j r", j=4),
+                    out=w0s[32 * q : 32 * q + 4, :, :].bitcast(I32),
+                    in_=w0_scales[:, 4 * q : 4 * q + 4, :].rearrange("g q n -> q g n").bitcast(I32),
                 )
 
-        load_x(0)
-        load_b(0)
-        load_x(1)
-        load_x(2)
-        load_x(3)
-        load_b(1)
-        for q in range(4):
-            nc.sync.dma_start(
-                out=wsc[32 * q : 32 * q + 4, 0:KG, :].bitcast(I32),
-                in_=w0_scales[:, 4 * q : 4 * q + 4, :].rearrange("g q n -> q g n").bitcast(I32),
-            )
-        for q in range(4):
-            nc.sync.dma_start(
-                out=wsc[32 * q : 32 * q + 4, KG, :].bitcast(I32),
-                in_=a_scales[0, 4 * q : 4 * q + 4, :].bitcast(I32),
-            )
-        nc.sync.dma_start(
-            out=w0[:].bitcast(I32),
-            in_=w0_words.rearrange("g p b -> p g b").bitcast(I32),
-        )
-        nc.sync.dma_start(out=aw[:].bitcast(I32), in_=a_words[0].bitcast(I32))
-        load_b(2)
-        load_b(3)
+        def load_a_scales():
+            for q in range(4):
+                nc.sync.dma_start(
+                    out=aws[32 * q : 32 * q + 4, :].bitcast(I32), in_=a_scales[0, 4 * q : 4 * q + 4, :].bitcast(I32)
+                )
 
-        grouped = {}
+        def interleave(m, g, on_vector, c0, c1):
+            if c1 > c0:
+                dst = bgr[m][:, g, :].rearrange("p (t c i j) -> p c t i j", t=4, i=2, j=4)
+                src = braw[(m, g)][:].rearrange("p j (c i t) -> p c t i j", i=2, t=4)
+                copy = nc.vector.tensor_copy if on_vector else nc.scalar.copy
+                copy(out=dst[:, c0:c1], in_=src[:, c0:c1])
 
-        def interleave(m, g):
-            tile_ = work.tile([P, 4 * R], BF16, name="grouped%d_%d" % (m, g), tag="grouped", bufs=6, align_bytes=64)
-            grouped[(m, g)] = tile_
-            v = VEC_T[m]
-            if isinstance(v, tuple):
-                v = v[g]
-            dst = tile_[:].rearrange("p (t c i j) -> p c t i j", t=4, i=2, j=4)
-            srcv = braw[m][:, g, :, :].rearrange("p j (c i t) -> p c t i j", i=2, t=4)
-            cut = 16 * v
-            if v < 4:
-                nc.scalar.copy(out=dst[:, cut:64], in_=srcv[:, cut:64])
-            if v > 0:
-                nc.vector.tensor_copy(out=dst[:, 0:cut], in_=srcv[:, 0:cut])
+        def inter_v(m, g):
+            interleave(m, g, True, 0, V_SHARE[m])
+
+        def inter_s(m, g, half=None):
+            c0, c1 = V_SHARE[m], 64
+            mid = (c0 + c1) // 2
+            if half == 0:
+                c1 = mid
+            if half == 1:
+                c0 = mid
+            interleave(m, g, False, c0, c1)
+
+        def warm(n):
+            bank = new_bank("warm", [P, P])
+            for k in range(n):
+                nc.tensor.matmul(bank[:], lhsT=ident[:], rhs=ident[:], start=True, stop=True)
+            release("warm")
 
         def quant_b(m, g):
-            nc.vector.quantize_mx(out=bq[m][:, g, :].bitcast(FP8X4), scales=bs[m][:, g, :], in_=grouped[(m, g)][:])
+            nc.vector.quantize_mx(out=bq[m][:, g, :].bitcast(FP8X4), scales=bs[m][:, g, :], in_=bgr[m][:, g, :])
 
-        def x_turn(i):
-            words = x_sb[:, i, :].bitcast(F32)
-            bank = bank_u("xt%d" % i, [P, KG, 2, P])
+        def mm_x(i):
+            words = x_sb[i][:].bitcast(F32)
+            bank = new_bank("xt%d" % i, [P, KG, 2, P])
+            held[("x", i)] = bank
             for g in range(KG):
                 for u in range(2):
                     nc.tensor.transpose(bank[:, g, u, :], words[:, 256 * g + u : 256 * (g + 1) : 2], ident[:])
-            dst = xg[:, :, P * i : P * (i + 1), :].rearrange("p g n t -> p g (n t)").bitcast(F32)
+
+        def drain_x(i):
+            bank = held.pop(("x", i))
+            release("xt%d" % i)
+            n = [n for n, (i0, i1) in enumerate(X_RUNS) if i0 <= i < i1][0]
+            sl = slice(P * (i - X_RUNS[n][0]), P * (i - X_RUNS[n][0] + 1))
+            dst = xg[n][:, :, sl, :].rearrange("p g n t -> p g (n t)").bitcast(F32)
             dst = dst.rearrange("p g (n u) -> p g n u", u=2)
             nc.scalar.copy(out=dst, in_=bank[:].rearrange("p g u n -> p g n u"))
 
-        def quant_x(i0, i1):
+        def quant_x(h):
+            sl = slice(P * X_RUNS[h][0], P * X_RUNS[h][1])
             for g in range(KG):
-                sl = slice(P * i0, P * i1)
                 nc.vector.quantize_mx(
                     out=xq[:, g, sl].bitcast(FP8X4),
                     scales=xs[:, g, sl],
-                    in_=xg[:, g, sl, :].rearrange("p n t -> p (n t)"),
+                    in_=xg[h][:, g, :, :].rearrange("p n t -> p (n t)"),
                 )
 
-        def stage1(m, i):
-            bank = bank_h("h%d_%d" % (m, i), [P, 4, P])
+        def gam_turn():
+            bank = new_bank("gam_bank", [P, P], BF16)
+            nc.tensor.transpose(bank[:], gam_rows[:], ident_b[:])
+            nc.scalar.copy(out=gam_t[:], in_=bank[:, 0 : NB * NJ])
+            release("gam_bank")
+
+        def mm_h(m, i):
+            bank = new_bank("h%d_%d" % (m, i), [P, 4, P])
+            held[("h", m, i)] = bank
             sl = slice(P * i, P * (i + 1))
             for t in range(4):
                 cols = slice(P * t, P * (t + 1))
@@ -169,6 +180,11 @@ def tile_randlorafullrankbasissum_x2_kernel(
                         start=(g == 0),
                         stop=(g == KG - 1),
                     )
+
+        def drain_h(m, i):
+            bank = held.pop(("h", m, i))
+            release("h%d_%d" % (m, i))
+            sl = slice(P * i, P * (i + 1))
             nc.vector.tensor_tensor(
                 out=hl[m][:, sl, :],
                 in0=bank[:].rearrange("p t n -> p n t"),
@@ -176,185 +192,290 @@ def tile_randlorafullrankbasissum_x2_kernel(
                 op=MULT,
             )
 
-        def quant_h(m, half):
-            sl = slice(256 * half, 256 * (half + 1))
+        def quant_h(m):
             nc.vector.quantize_mx(
-                out=hq[m][:, sl].bitcast(FP8X4), scales=hs[m][:, sl], in_=hl[m][:, sl, :].rearrange("p n t -> p (n t)")
+                out=hq[m][:].bitcast(FP8X4), scales=hs[m][:], in_=hl[m][:].rearrange("p n t -> p (n t)")
             )
 
-        def base(j):
-            bank = bank_u("base%d" % j, [P, TOK])
+        def mm_base(j):
+            bank = new_bank("base%d" % j, [P, TOK])
+            held[("base", j)] = bank
             for g in range(KG):
                 nc.tensor.matmul_mx(
                     out=bank[:],
                     lhsT=w0[:, g, 256 * j : 256 * (j + 1)].bitcast(FP4X4),
-                    lhsT_scale=wsc[:, g, P * j : P * (j + 1)],
+                    lhsT_scale=w0s[:, g, P * j : P * (j + 1)],
                     rhs=xq[:, g, :].bitcast(FP8X4),
                     rhs_scale=xs[:, g, :],
                     start=(g == 0),
                     stop=(g == KG - 1),
                 )
-            copy = nc.vector.tensor_copy if j in VEC_BASE else nc.scalar.copy
-            copy(out=acc[:, j, :], in_=bank[:])
 
-        def stage2(m, j):
-            bank = bank_u("u%d_%d" % (m, j), [P, TOK])
+        def drain_base(j):
+            bank = held.pop(("base", j))
+            release("base%d" % j)
+            piece = sb("part_base%d" % j, [P, TOK], F32)
+            nc.scalar.copy(out=piece[:], in_=bank[:])
+            parts[j].append(piece)
+
+        def mm_u(m, j):
+            bank = new_bank("u%d_%d" % (m, j), [P, TOK])
+            held[("u", m, j)] = bank
             nc.tensor.matmul_mx(
                 out=bank[:],
                 lhsT=aw[:, 256 * j : 256 * (j + 1)].bitcast(FP4X4),
-                lhsT_scale=wsc[:, KG, P * j : P * (j + 1)],
+                lhsT_scale=aws[:, P * j : P * (j + 1)],
                 rhs=hq[m][:].bitcast(FP8X4),
                 rhs_scale=hs[m][:],
                 start=True,
                 stop=True,
             )
-            col = gam_t[:, NJ * m + j : NJ * m + j + 1]
-            if (m, j) in S_U:
-                nc.scalar.activation(out=part[(m, j)][:], in_=bank[:], func=COPY, scale=col)
-            else:
-                nc.vector.scalar_tensor_tensor(
-                    out=acc[:, j, :], in0=bank[:], scalar=col, in1=acc[:, j, :], op0=MULT, op1=ADD
-                )
 
-        def out_bank(j):
-            bank = bank_h("o%d" % j, [P, TT, P])
-            parts = [part[key][:] for key in sorted(part) if key[1] == j] + [acc[:, j, :]]
-            for i in range(TT):
-                for n, piece in enumerate(parts):
+        def drain_u(m, j, on_vector):
+            bank = held.pop(("u", m, j))
+            release("u%d_%d" % (m, j))
+            col = gam_t[:, NJ * m + j : NJ * m + j + 1]
+            if on_vector and not parts[j]:
+                piece = sb("part%d_%d" % (m, j), [P, TOK], F32)
+                nc.vector.tensor_scalar(out=piece[:], in0=bank[:], scalar1=col, scalar2=None, op0=MULT)
+                parts[j].append(piece)
+            elif on_vector:
+                acc = parts[j][0]
+                nc.vector.scalar_tensor_tensor(out=acc[:], in0=bank[:], scalar=col, in1=acc[:], op0=MULT, op1=ADD)
+            else:
+                piece = sb("part%d_%d" % (m, j), [P, TOK], F32)
+                nc.scalar.activation(out=piece[:], in_=bank[:], func=COPY, scale=col)
+                parts[j].append(piece)
+
+        def pool_add(j):
+            last = parts[j].pop()
+            acc = parts[j][-1]
+            nc.gpsimd.tensor_tensor(out=acc[:], in0=acc[:], in1=last[:], op=ADD)
+
+        def turn_parts(j, last, keep_first=False):
+            first = j not in out_bank
+            if first:
+                out_bank[j] = new_bank("o%d" % j, [P, TT, P])
+            order = list(reversed(parts[j][1:] if keep_first else parts[j]))
+            kept = parts[j][:1] if keep_first else []
+            parts[j].clear()
+            parts[j].extend(kept)
+            for n, piece in enumerate(order):
+                for i in range(TT):
                     nc.tensor.matmul(
-                        bank[:, i, :],
+                        out_bank[j][:, i, :],
                         lhsT=piece[:, P * i : P * (i + 1)],
                         rhs=ident[:],
-                        start=(n == 0),
-                        stop=(n == len(parts) - 1),
+                        start=(first and n == 0 and i == 0),
+                        stop=(last and n == len(order) - 1 and i == TT - 1),
                         is_transpose=True,
                     )
-            cols = slice(P * j, P * (j + 1))
-            copy = nc.vector.tensor_copy if j in VEC_OUT else nc.scalar.copy
-            copy(out=o32[:, :, cols], in_=bank[:])
+
+        def drain_out(j, on_vector=False):
+            bank = out_bank[j]
+            release("o%d" % j)
+            copy = nc.vector.tensor_copy if on_vector else nc.scalar.copy
+            copy(out=o32[j // 2][:, :, P * (j % 2) : P * (j % 2 + 1)], in_=bank[:])
 
         def store(j0, j1):
-            cols = slice(P * j0, P * j1)
-            nc.sync.dma_start(out=out_0[:, cols].rearrange("(i p) f -> p i f", p=P), in_=o32[:, :, cols])
+            nc.sync.dma_start(
+                out=out_0[:, P * j0 : P * j1].rearrange("(i p) f -> p i f", p=P),
+                in_=o32[j0 // 2][:, :, P * (j0 % 2) : P * (j0 % 2 + j1 - j0)],
+            )
 
-        def round_out(j):
-            h, jj = j // 4, j % 4
-            dst = o16[:].rearrange("p i (h u q e) -> p i h u q e", h=2, u=2, e=2)[:, :, h, :, 32 * jj : 32 * (jj + 1), :]
-            src = o32[:, :, P * j : P * (j + 1)].rearrange("p i (q u e) -> p i u q e", u=2, e=2)
-            if j in G_CAST:
-                nc.gpsimd.tensor_scalar(out=dst, in0=src, scalar1=1.0, scalar2=-0.0, op0=MULT, op1=ADD)
-            else:
-                nc.vector.tensor_copy(out=dst, in_=src)
+        def round_out(j0, j1, on_vector=True):
+            q0 = 32 * (j0 % 4)
+            dst = o16[j0 // 4][:].rearrange("p i (u q e) -> p i u q e", u=2, e=2)[:, :, :, q0 : q0 + 32 * (j1 - j0), :]
+            src = o32[j0 // 2][:, :, P * (j0 % 2) : P * (j0 % 2 + j1 - j0)].rearrange("p i (q u e) -> p i u q e", u=2, e=2)
+            copy = nc.vector.tensor_copy if on_vector else nc.scalar.copy
+            copy(out=dst, in_=src)
 
-        def plane_turn(h, ip):
-            bank = bank_h("pt%d_%d" % (h, ip), [P, 2, 2, P])
+        def mm_plane(g, h):
+            bank = new_bank("pt%d_%d" % (g, h), [P, 2, 2, P])
+            held[("plane", g, h)] = bank
             for ii in range(2):
-                words = o16[:, 2 * ip + ii, :].bitcast(F32)
+                words = o16[g][:, 2 * h + ii, :].bitcast(F32)
                 for u in range(2):
-                    w = 256 * h + 128 * u
-                    nc.tensor.transpose(bank[:, ii, u, :], words[:, w : w + 128], ident[:])
-            sl = slice(256 * ip, 256 * (ip + 1))
-            dst = pg[:, h, sl, :].rearrange("p n t -> p (n t)").bitcast(F32)
+                    nc.tensor.transpose(bank[:, ii, u, :], words[:, P * u : P * (u + 1)], ident[:])
+
+        def drain_plane(g, h, on_vector=False):
+            bank = held.pop(("plane", g, h))
+            release("pt%d_%d" % (g, h))
+            dst = pg[(g, h)][:].rearrange("p n t -> p (n t)").bitcast(F32)
             dst = dst.rearrange("p (i n u) -> p i n u", i=2, u=2)
-            copy = nc.vector.tensor_copy if 2 * h + ip in VEC_PL else nc.scalar.copy
+            copy = nc.vector.tensor_copy if on_vector else nc.scalar.copy
             copy(out=dst, in_=bank[:].rearrange("p i u n -> p i n u"))
 
-        def plane_quant(h, ip):
-            sl = slice(256 * ip, 256 * (ip + 1))
+        def plane_quant(g, h):
+            sl = slice(256 * h, 256 * (h + 1))
             nc.vector.quantize_mx(
-                out=pq[:, h, sl].bitcast(FP8X4), scales=ps[:, h, sl], in_=pg[:, h, sl, :].rearrange("p n t -> p (n t)")
-            )
-            nc.sync.dma_start(
-                out=out_1[h].rearrange("p n t -> p (n t)").bitcast(I32)[:, sl], in_=pq[:, h, sl].bitcast(I32)
+                out=pq[g][:, sl].bitcast(FP8X4), scales=ps[4 * g : P, sl], in_=pg[(g, h)][:].rearrange("p n t -> p (n t)")
             )
 
-        def plane_scales(h):
+        def plane_store(g):
+            nc.sync.dma_start(out=out_1[g].rearrange("p n t -> p (n t)").bitcast(I32), in_=pq[g][:].bitcast(I32))
+
+        def scale_store():
             for q in range(4):
                 eng = nc.sync if q % 2 == 0 else nc.scalar
                 eng.dma_start(
-                    out=out_2[h, 4 * q : 4 * q + 4, :].bitcast(I32), in_=ps[32 * q : 32 * q + 4, h, :].bitcast(I32)
+                    out=out_2[:, 4 * q : 4 * q + 4, :].bitcast(I32), in_=ps[32 * q : 32 * q + 8, :].bitcast(I32)
                 )
 
-        def compute():
-            x_turn(0)
-            vbank = bank_u("vbank", [P, 5, P], BF16)
-            for t in range(4):
-                nc.tensor.transpose(vbank[:, t, :], vec[:, t:R:4], ident_b[:])
-            nc.tensor.transpose(vbank[:, 4, :], vec[:, R : R + P], ident_b[:])
-            interleave(0, 0)
-            quant_x(0, 1)
-            interleave(0, 1)
-            quant_b(0, 0)
-            nc.scalar.copy(
-                out=lam_t[:].rearrange("p m o t -> p m (o t)"), in_=vbank[:, 0:4, 0:NB].rearrange("p t m -> p m t")
-            )
-            nc.scalar.copy(out=gam_t[:], in_=vbank[:, 4, 0 : NB * NJ])
-            x_turn(1)
-            quant_b(0, 1)
-            quant_x(1, 2)
-            x_turn(2)
-            x_turn(3)
-            quant_x(2, 4)
-            for s in range(NB + 1):
-                for i in range(4):
-                    if s < NB:
-                        stage1(s, i)
-                    if s + 1 < NB and i < 2:
-                        interleave(s + 1, i)
-                    if s == 1:
-                        base(i)
-                    if s > 0:
-                        stage2(s - 1, i)
-                    if s < NB and i == 2:
-                        quant_h(s, 0)
-                    if s + 1 < NB and i > 1:
-                        quant_b(s + 1, i - 2)
-                if s < NB:
-                    quant_h(s, 1)
-                if PH2 and s > 1:
-                    for j in range(4, 4 + PH2):
-                        if s == 2:
-                            base(j)
-                        stage2(s - 2, j)
-            for j in range(4 + PH2, 8):
-                base(j)
-            for pair in ((4, 5), (6, 7)):
-                for m in range(NB):
-                    for j in pair:
-                        if j >= 4 + PH2 or m == NB - 1:
-                            stage2(m, j)
-                    if pair[0] == 4:
-                        out_bank(m)
-                        if m in (1, 3):
-                            store(m - 1, m + 1)
-                        round_out(m)
-                    if pair[0] == 6:
-                        if m == 0:
-                            plane_turn(0, 0)
-                            plane_turn(0, 1)
-                        if m == 1:
-                            plane_quant(0, 0)
-                            plane_quant(0, 1)
-                            plane_scales(0)
-                        if m == 2:
-                            out_bank(4)
-                            round_out(4)
-                        if m == 3:
-                            out_bank(5)
-                            store(4, 6)
-                            round_out(5)
-            for j in (6, 7):
-                out_bank(j)
-                store(j, j + 1)
-                round_out(j)
-            plane_turn(1, 0)
-            plane_turn(1, 1)
-            plane_quant(1, 0)
-            plane_quant(1, 1)
-            plane_scales(1)
+        def stage1(m, i):
+            mm_h(m, i)
+            drain_h(m, i)
 
-        if MANUAL:
-            with tc.manual_schedule():
-                compute()
-        else:
-            compute()
+        def stage2(m, j, on_vector):
+            mm_u(m, j)
+            drain_u(m, j, on_vector)
+
+        def base(j):
+            mm_base(j)
+            drain_base(j)
+
+        def x_turn(i):
+            mm_x(i)
+            drain_x(i)
+
+        def out_turn(j, on_vector=False):
+            turn_parts(j, True)
+            drain_out(j, on_vector)
+
+        def plane_turn(g, h, on_vector=False):
+            mm_plane(g, h)
+            drain_plane(g, h, on_vector)
+
+        make_identity(nc, ident[:])
+        nc.vector.memset(gam_rows[:], 0.0)
+        nc.vector.memset(w0s[:].rearrange("p g n -> p (g n)").bitcast(I32), 0)
+        nc.vector.memset(aws[:].bitcast(I32), 0)
+        nc.scalar.dma_start(
+            out=lam_t[:].rearrange("p m o t -> p m (o t)"), in_=lam.rearrange("m (p t) -> p m t", t=4)
+        )
+        nc.scalar.dma_start(out=gam_rows[0 : NB * NJ, :], in_=gam.rearrange("m (j p) -> (m j) p", p=P))
+        nc.scalar.activation(out=ident_b[:], in_=ident[:], func=COPY)
+        load_b(0, 0)
+        load_x(0)
+        load_b(0, 1)
+        load_x(1)
+        load_x(2)
+        load_x(3)
+        load_b(1, 0)
+        load_b(1, 1)
+        load_w0_scales()
+        nc.sync.dma_start(out=w0[:].bitcast(I32), in_=w0_words.rearrange("g p b -> p g b").bitcast(I32))
+        nc.sync.dma_start(out=aw[:].bitcast(I32), in_=a_words[0].bitcast(I32))
+        load_a_scales()
+        for m in range(2, NB):
+            for g in range(KG):
+                load_b(m, g)
+
+        inter_s(0, 0)
+        inter_v(0, 0)
+        quant_b(0, 0)
+        x_turn(0)
+        inter_s(0, 1)
+        inter_v(0, 1)
+        quant_x(0)
+        quant_b(0, 1)
+        x_turn(1)
+        quant_x(1)
+        x_turn(2)
+        x_turn(3)
+        mm_h(0, 0)
+        mm_h(0, 1)
+        inter_v(1, 0)
+        inter_s(1, 0)
+        quant_x(2)
+        drain_h(0, 0)
+        drain_h(0, 1)
+        mm_h(0, 2)
+        mm_h(0, 3)
+        inter_v(1, 1)
+        inter_s(1, 1)
+        gam_turn()
+        quant_b(1, 0)
+        drain_h(0, 2)
+        quant_b(1, 1)
+        drain_h(0, 3)
+        base(0)
+        base(1)
+
+        for m in range(1, NB):
+            more = m + 1 < NB
+            stage1(m, 0)
+            quant_h(m - 1)
+            if m == 1:
+                base(2)
+                base(3)
+            stage1(m, 1)
+            stage1(m, 2)
+            if more:
+                inter_s(m + 1, 0)
+                inter_v(m + 1, 0)
+                inter_s(m + 1, 1)
+            if m == 3:
+                stage2(1, 4, False)
+                stage2(1, 5, False)
+            stage2(m - 1, 0, True)
+            stage2(m - 1, 1, True)
+            if more:
+                inter_v(m + 1, 1)
+                quant_b(m + 1, 0)
+            if m == 3:
+                stage2(1, 6, False)
+                stage2(1, 7, False)
+            stage1(m, 3)
+            if more:
+                quant_b(m + 1, 1)
+            stage2(m - 1, 2, True)
+            stage2(m - 1, 3, True)
+            for j in range(4, 8):
+                if m == 1:
+                    base(j)
+                if m == 2:
+                    stage2(0, j, False)
+
+        stage2(2, 7, False)
+        stage2(2, 6, False)
+        quant_h(3)
+        stage2(2, 4, True)
+        turn_parts(4, False, True)
+        turn_parts(5, False, True)
+        for j in range(4):
+            stage2(3, j, True)
+        stage2(2, 5, True)
+        out_turn(0)
+        out_turn(1)
+        store(0, 2)
+        stage2(3, 4, True)
+        stage2(3, 5, True)
+        out_turn(2)
+        out_turn(3)
+        store(2, 4)
+        round_out(0, 2, False)
+        stage2(3, 6, True)
+        stage2(3, 7, True)
+        round_out(2, 4, True)
+        turn_parts(6, False, True)
+        out_turn(4)
+        out_turn(5, True)
+        store(4, 6)
+        turn_parts(7, False, True)
+        plane_turn(0, 0)
+        out_turn(6)
+        round_out(4, 6)
+        out_turn(7, True)
+        store(6, 8)
+        plane_turn(0, 1)
+        round_out(6, 8)
+        plane_quant(0, 0)
+        plane_turn(1, 0)
+        plane_quant(0, 1)
+        plane_store(0)
+        plane_turn(1, 1, True)
+        plane_quant(1, 0)
+        plane_quant(1, 1)
+        plane_store(1)
+        scale_store()

@@ -21,14 +21,15 @@ P = 128
 KG = D // 512
 TT = TOK // P
 NJ = F // P
-X_RUNS = ((0, 1), (1, 2), (2, 4))
-V_SHARE = (40,24,8,8)
-V_J = (0, 1, 2, 3, 4)
-S_J = (5, 6, 7)
-HELD = (5, 6, 7)
-BASE_AT = {1: (5,), 2: (6,), 3: (7,)}
-S_LAST = (1,)
-LAG = 3
+X_RUNS = ((0, 2), (2, 4))
+V_SHARE = ((0, 64), (0, 40), (0, 32), (0, 32))
+BASE_AT = ((0,), (1, 2), (3, 4, 5, 6, 7), ())
+EARLY = ((), (), ((0, 0), (1, 0)), ((1, 2), (0, 3)))
+MID = ((), (), (), ((0, 1), (0, 2)))
+LATE = (((0, 4), (1,4), (0, 5)), ((0, 6), (0, 7)), ())
+BASE_MM = ((0,), (1, 2, 3, 4), (5, 6, 7), ())
+AHEAD = 4
+ON_SCALAR = [unit for group in EARLY + MID + LATE for unit in group]
 
 
 def tile_randlorafullrankbasissum_x2_kernel(
@@ -112,10 +113,10 @@ def tile_randlorafullrankbasissum_x2_kernel(
                 copy(out=dst[:, c0:c1], in_=src[:, c0:c1])
 
         def inter_v(m, g):
-            interleave(m, g, True, 0, V_SHARE[m])
+            interleave(m, g, True, 0, V_SHARE[m][g])
 
         def inter_s(m, g, half=None):
-            c0, c1 = V_SHARE[m], 64
+            c0, c1 = V_SHARE[m][g], 64
             mid = (c0 + c1) // 2
             if half == 0:
                 c1 = mid
@@ -312,8 +313,11 @@ def tile_randlorafullrankbasissum_x2_kernel(
                 out=pq[g][:, sl].bitcast(FP8X4), scales=ps[4 * g : P, sl], in_=pg[(g, h)][:].rearrange("p n t -> p (n t)")
             )
 
-        def plane_store(g):
-            nc.sync.dma_start(out=out_1[g].rearrange("p n t -> p (n t)").bitcast(I32), in_=pq[g][:].bitcast(I32))
+        def plane_store(g, h0=0, h1=2):
+            sl = slice(256 * h0, 256 * h1)
+            nc.sync.dma_start(
+                out=out_1[g].rearrange("p n t -> p (n t)").bitcast(I32)[:, sl], in_=pq[g][:, sl].bitcast(I32)
+            )
 
         def scale_store():
             for q in range(4):
@@ -373,109 +377,104 @@ def tile_randlorafullrankbasissum_x2_kernel(
 
         inter_s(0, 0)
         inter_v(0, 0)
-        quant_b(0, 0)
         x_turn(0)
         inter_s(0, 1)
         inter_v(0, 1)
-        quant_x(0)
+        quant_b(0, 0)
         quant_b(0, 1)
         x_turn(1)
-        quant_x(1)
+        quant_x(0)
         x_turn(2)
         x_turn(3)
-        mm_h(0, 0)
-        mm_h(0, 1)
         inter_v(1, 0)
         inter_s(1, 0)
-        quant_x(2)
-        drain_h(0, 0)
-        drain_h(0, 1)
-        mm_h(0, 2)
-        mm_h(0, 3)
-        inter_v(1, 1)
         inter_s(1, 1)
+        inter_v(1, 1)
+        quant_x(1)
         gam_turn()
-        quant_b(1, 0)
-        drain_h(0, 2)
-        quant_b(1, 1)
-        drain_h(0, 3)
-        base(0)
-        base(1)
 
-        for m in range(1, NB):
+        for m in range(NB):
             more = m + 1 < NB
-            stage1(m, 0)
-            quant_h(m - 1)
-            if m == 1:
-                base(2)
-                base(3)
-            stage1(m, 1)
-            stage1(m, 2)
-            if more:
-                inter_s(m + 1, 0)
-                inter_v(m + 1, 0)
-                inter_s(m + 1, 1)
-            if m == 3:
-                stage2(1, 4, False)
-                stage2(1, 5, False)
-            stage2(m - 1, 0, True)
-            stage2(m - 1, 1, True)
-            if more:
+            mm_h(m, 0)
+            mm_h(m, 1)
+            for term, j in MID[m]:
+                stage2(term, j, False)
+            mm_h(m, 2)
+            mm_h(m, 3)
+            drain_h(m, 0)
+            if m > 0:
+                quant_h(m - 1)
+            if more and m > 0:
                 inter_v(m + 1, 1)
-                quant_b(m + 1, 0)
-            if m == 3:
-                stage2(1, 6, False)
-                stage2(1, 7, False)
-            stage1(m, 3)
+            drain_h(m, 1)
             if more:
+                quant_b(m + 1, 0)
                 quant_b(m + 1, 1)
-            stage2(m - 1, 2, True)
-            stage2(m - 1, 3, True)
-            for j in range(4, 8):
-                if m == 1:
-                    base(j)
-                if m == 2:
-                    stage2(0, j, False)
+            for j in BASE_MM[m]:
+                mm_base(j)
+            for j in BASE_AT[m]:
+                drain_base(j)
+            if m + 2 < NB:
+                inter_s(m + 2, 0)
+                inter_s(m + 2, 1)
+            drain_h(m, 2)
+            drain_h(m, 3)
+            for term, j in EARLY[m]:
+                stage2(term, j, False)
 
-        stage2(2, 7, False)
-        stage2(2, 6, False)
+        stream = [(term, j + k) for j in range(0, NJ, 2) for term in range(NB) for k in range(2)]
+        stream = [unit for unit in stream if unit not in ON_SCALAR]
+
+        def vec(n):
+            for k in range(n):
+                term, j = stream.pop(0)
+                stage2(term, j, True)
+
+        def upto(unit, more):
+            vec(stream.index(unit) + 1 + more)
+
+        vec(1)
         quant_h(3)
-        stage2(2, 4, True)
-        turn_parts(4, False, True)
-        turn_parts(5, False, True)
-        for j in range(4):
-            stage2(3, j, True)
-        stage2(2, 5, True)
+        vec(2)
+        for term, j in LATE[0]:
+            stage2(term, j, False)
+        upto((3, 1), 0)
+        for term, j in LATE[1]:
+            stage2(term, j, False)
+        vec(AHEAD)
         out_turn(0)
         out_turn(1)
         store(0, 2)
-        stage2(3, 4, True)
-        stage2(3, 5, True)
+        upto((3, 3), AHEAD)
+        round_out(0, 2, False)
         out_turn(2)
         out_turn(3)
         store(2, 4)
-        round_out(0, 2, False)
-        stage2(3, 6, True)
-        stage2(3, 7, True)
-        round_out(2, 4, True)
-        turn_parts(6, False, True)
+        upto((3, 5), AHEAD)
+        round_out(2, 4, False)
         out_turn(4)
-        out_turn(5, True)
+        out_turn(5)
         store(4, 6)
-        turn_parts(7, False, True)
+        for term, j in LATE[2]:
+            stage2(term, j, False)
+        vec(len(stream))
+        round_out(4, 6, False)
         plane_turn(0, 0)
+        turn_parts(6, False, True)
+        turn_parts(7, False, True)
         out_turn(6)
-        round_out(4, 6)
         out_turn(7, True)
         store(6, 8)
         plane_turn(0, 1)
-        round_out(6, 8)
+        round_out(6, 7)
+        round_out(7, 8)
         plane_quant(0, 0)
         plane_turn(1, 0)
         plane_quant(0, 1)
         plane_store(0)
         plane_turn(1, 1, True)
         plane_quant(1, 0)
+        plane_store(1, 0, 1)
         plane_quant(1, 1)
-        plane_store(1)
+        plane_store(1, 1, 2)
         scale_store()

@@ -22,14 +22,15 @@ KG = D // 512
 TT = TOK // P
 NJ = F // P
 X_RUNS = ((0, 2), (2, 4))
-V_SHARE = ((0, 64), (0, 40), (0, 32), (0, 32))
+V_SHARE = ((0, 64), (0, 56), (0, 48), (0, 48))
 BASE_AT = ((0,), (1, 2), (3, 4, 5, 6, 7), ())
 EARLY = ((), (), ((0, 0), (1, 0)), ((1, 2), (0, 3)))
 MID = ((), (), (), ((0, 1), (0, 2)))
-LATE = (((0, 4), (1,4), (0, 5)), ((0, 6), (0, 7)), ())
+LATE = (((0, 4), (1, 4), (0, 5)), ((0, 6), (0, 7)), ())
 BASE_MM = ((0,), (1, 2, 3, 4), (5, 6, 7), ())
 AHEAD = 4
 ON_SCALAR = [unit for group in EARLY + MID + LATE for unit in group]
+WALK = (1, 0)
 
 
 def tile_randlorafullrankbasissum_x2_kernel(
@@ -68,6 +69,7 @@ def tile_randlorafullrankbasissum_x2_kernel(
         w0s = sb("w0s", [P, KG, F], U8)
         aws = sb("aws", [P, F], U8)
         gam_rows = sb("gam_rows", [P, P], BF16)
+        lam_rows = sb("lam_rows", [P, R // 2], F32)
         ident = sb("ident", [P, P], F32)
         ident_b = sb("ident_b", [P, P], BF16)
         lam_t = sb("lam_t", [P, NB, 1, 4], BF16)
@@ -107,10 +109,15 @@ def tile_randlorafullrankbasissum_x2_kernel(
 
         def interleave(m, g, on_vector, c0, c1):
             if c1 > c0:
-                dst = bgr[m][:, g, :].rearrange("p (t c i j) -> p c t i j", t=4, i=2, j=4)
-                src = braw[(m, g)][:].rearrange("p j (c i t) -> p c t i j", i=2, t=4)
                 copy = nc.vector.tensor_copy if on_vector else nc.scalar.copy
-                copy(out=dst[:, c0:c1], in_=src[:, c0:c1])
+                if WALK[on_vector] == 0:
+                    dst = bgr[m][:, g, :].rearrange("p (t c i j) -> p c t i j", t=4, i=2, j=4)
+                    src = braw[(m, g)][:].rearrange("p j (c i t) -> p c t i j", i=2, t=4)
+                    copy(out=dst[:, c0:c1], in_=src[:, c0:c1])
+                else:
+                    dst = bgr[m][:, g, :].rearrange("p (t n j) -> p n j t", t=4, j=4)
+                    src = braw[(m, g)][:].rearrange("p j (n t) -> p n j t", t=4)
+                    copy(out=dst[:, 2 * c0 : 2 * c1], in_=src[:, 2 * c0 : 2 * c1])
 
         def inter_v(m, g):
             interleave(m, g, True, 0, V_SHARE[m][g])
@@ -158,6 +165,14 @@ def tile_randlorafullrankbasissum_x2_kernel(
                     scales=xs[:, g, sl],
                     in_=xg[h][:, g, :, :].rearrange("p n t -> p (n t)"),
                 )
+
+        def lam_turn():
+            bank = new_bank("lam_bank", [P, 2, P])
+            for u in range(2):
+                nc.tensor.transpose(bank[:, u, :], lam_rows[:, u : R // 2 : 2], ident[:])
+            dst = lam_t[:].rearrange("p m o t -> p m (o t)").bitcast(F32)
+            nc.vector.tensor_copy(out=dst, in_=bank[:, :, 0:NB].rearrange("p u m -> p m u"))
+            release("lam_bank")
 
         def gam_turn():
             bank = new_bank("gam_bank", [P, P], BF16)
@@ -350,13 +365,12 @@ def tile_randlorafullrankbasissum_x2_kernel(
             mm_plane(g, h)
             drain_plane(g, h, on_vector)
 
-        make_identity(nc, ident[:])
+        nc.vector.memset(lam_rows[:], 0.0)
         nc.vector.memset(gam_rows[:], 0.0)
+        make_identity(nc, ident[:])
         nc.vector.memset(w0s[:].rearrange("p g n -> p (g n)").bitcast(I32), 0)
         nc.vector.memset(aws[:].bitcast(I32), 0)
-        nc.scalar.dma_start(
-            out=lam_t[:].rearrange("p m o t -> p m (o t)"), in_=lam.rearrange("m (p t) -> p m t", t=4)
-        )
+        nc.scalar.dma_start(out=lam_rows[0:NB, :].bitcast(BF16), in_=lam[:, :])
         nc.scalar.dma_start(out=gam_rows[0 : NB * NJ, :], in_=gam.rearrange("m (j p) -> (m j) p", p=P))
         nc.scalar.activation(out=ident_b[:], in_=ident[:], func=COPY)
         load_b(0, 0)
@@ -375,6 +389,7 @@ def tile_randlorafullrankbasissum_x2_kernel(
             for g in range(KG):
                 load_b(m, g)
 
+        lam_turn()
         inter_s(0, 0)
         inter_v(0, 0)
         x_turn(0)

@@ -22,12 +22,12 @@ KG = D // 512
 TT = TOK // P
 NJ = F // P
 X_RUNS = ((0, 2), (2, 4))
-V_SHARE = ((0, 64), (0, 56), (0, 48), (0, 48))
-BASE_AT = ((0,), (1, 2), (3, 4, 5, 6, 7), ())
+V_SHARE = ((0, 64), (0, 48), (0, 32), (0, 48))
+BASE_AT = ((), (0,1), (2,3,4,5,6,7), ())
 EARLY = ((), (), ((0, 0), (1, 0)), ((1, 2), (0, 3)))
 MID = ((), (), (), ((0, 1), (0, 2)))
 LATE = (((0, 4), (1, 4), (0, 5)), ((0, 6), (0, 7)), ())
-BASE_MM = ((0,), (1, 2, 3, 4), (5, 6, 7), ())
+BASE_MM = ((), (0,1,2,3), (4,5,6,7), ())
 AHEAD = 4
 ON_SCALAR = [unit for group in EARLY + MID + LATE for unit in group]
 WALK = (1, 0)
@@ -78,7 +78,7 @@ def tile_randlorafullrankbasissum_x2_kernel(
         hq = [sb("hq%d" % m, [P, TOK], U32) for m in range(NB)]
         hs = [sb("hs%d" % m, [P, TOK], U8) for m in range(NB)]
         o32 = [sb("o32_%d" % jp, [P, TT, 2 * P], F32) for jp in range(NJ // 2)]
-        o16 = [sb("o16_%d" % g, [P, TT, 512], BF16) for g in range(2)]
+        o16 = [sb("o16_%d" % g, [P, 2, TT, 256], BF16) for g in range(2)]
         pg = {(g, h): sb("pg%d_%d" % (g, h), [P, 256, 4], BF16) for g in range(2) for h in range(2)}
         pq = [sb("pq%d" % g, [P, TOK], U32) for g in range(2)]
         ps = sb("ps", [P, TOK], U8)
@@ -263,10 +263,14 @@ def tile_randlorafullrankbasissum_x2_kernel(
                 nc.scalar.activation(out=piece[:], in_=bank[:], func=COPY, scale=col)
                 parts[j].append(piece)
 
-        def pool_add(j):
+        def pool_add(j, fresh=False):
             last = parts[j].pop()
-            acc = parts[j][-1]
-            nc.gpsimd.tensor_tensor(out=acc[:], in0=acc[:], in1=last[:], op=ADD)
+            acc = parts[j][0]
+            total = acc
+            if fresh:
+                total = keep.tile([P, TOK], F32, name="sum%d" % j, tag="hl3", align_bytes=64)
+                parts[j][0] = total
+            nc.gpsimd.tensor_tensor(out=total[:], in0=acc[:], in1=last[:], op=ADD)
 
         def turn_parts(j, last, keep_first=False):
             first = j not in out_bank
@@ -301,18 +305,20 @@ def tile_randlorafullrankbasissum_x2_kernel(
 
         def round_out(j0, j1, on_vector=True):
             q0 = 32 * (j0 % 4)
-            dst = o16[j0 // 4][:].rearrange("p i (u q e) -> p i u q e", u=2, e=2)[:, :, :, q0 : q0 + 32 * (j1 - j0), :]
-            src = o32[j0 // 2][:, :, P * (j0 % 2) : P * (j0 % 2 + j1 - j0)].rearrange("p i (q u e) -> p i u q e", u=2, e=2)
-            copy = nc.vector.tensor_copy if on_vector else nc.scalar.copy
-            copy(out=dst, in_=src)
+            dst = o16[j0 // 4][:].rearrange("p u i (q e) -> p u i q e", e=2)[:, :, :, q0 : q0 + 32 * (j1 - j0), :]
+            src = o32[j0 // 2][:, :, P * (j0 % 2) : P * (j0 % 2 + j1 - j0)].rearrange("p i (q u e) -> p u i q e", u=2, e=2)
+            if on_vector == 2:
+                nc.gpsimd.tensor_scalar(out=dst, in0=src, scalar1=1.0, scalar2=-0.0, op0=MULT, op1=ADD)
+            else:
+                copy = nc.vector.tensor_copy if on_vector else nc.scalar.copy
+                copy(out=dst, in_=src)
 
         def mm_plane(g, h):
             bank = new_bank("pt%d_%d" % (g, h), [P, 2, 2, P])
             held[("plane", g, h)] = bank
             for ii in range(2):
-                words = o16[g][:, 2 * h + ii, :].bitcast(F32)
                 for u in range(2):
-                    nc.tensor.transpose(bank[:, ii, u, :], words[:, P * u : P * (u + 1)], ident[:])
+                    nc.tensor.transpose(bank[:, ii, u, :], o16[g][:, u, 2 * h + ii, :].bitcast(F32), ident[:])
 
         def drain_plane(g, h, on_vector=False):
             bank = held.pop(("plane", g, h))
@@ -381,13 +387,14 @@ def tile_randlorafullrankbasissum_x2_kernel(
         load_x(3)
         load_b(1, 0)
         load_b(1, 1)
+        load_b(2, 0)
+        load_b(2, 1)
         load_w0_scales()
         nc.sync.dma_start(out=w0[:].bitcast(I32), in_=w0_words.rearrange("g p b -> p g b").bitcast(I32))
-        nc.sync.dma_start(out=aw[:].bitcast(I32), in_=a_words[0].bitcast(I32))
+        load_b(3, 0)
+        load_b(3, 1)
         load_a_scales()
-        for m in range(2, NB):
-            for g in range(KG):
-                load_b(m, g)
+        nc.sync.dma_start(out=aw[:].bitcast(I32), in_=a_words[0].bitcast(I32))
 
         lam_turn()
         inter_s(0, 0)

@@ -22,11 +22,11 @@ KG = D // 512
 TT = TOK // P
 NJ = F // P
 X_RUNS = ((0, 2), (2, 4))
-V_SHARE = ((0, 64), (0, 48), (0, 32), (0, 48))
+V_SHARE = ((0, 64), (0, 48), (0, 32), (0, 40))
 BASE_AT = ((), (0,1), (2,3,4,5,6,7), ())
-EARLY = ((), (), ((0, 0), (1, 0)), ((1, 2), (0, 3)))
+EARLY = ((), (), ((0, 0),), ((0, 3),))
 MID = ((), (), (), ((0, 1), (0, 2)))
-LATE = (((0, 4), (1, 4), (0, 5)), ((0, 6), (0, 7)), ())
+LATE = (((0,4),(0,5)),((0,6),(0,7),(1,6),(1,7)),())
 BASE_MM = ((), (0,1,2,3), (4,5,6,7), ())
 AHEAD = 4
 ON_SCALAR = [unit for group in EARLY + MID + LATE for unit in group]
@@ -457,12 +457,16 @@ def tile_randlorafullrankbasissum_x2_kernel(
 
         vec(1)
         quant_h(3)
+        pool_add(2, True)
+        pool_add(3)
         vec(2)
         for term, j in LATE[0]:
             stage2(term, j, False)
+            pool_add(j)
         upto((3, 1), 0)
         for term, j in LATE[1]:
             stage2(term, j, False)
+            pool_add(j)
         vec(AHEAD)
         out_turn(0)
         out_turn(1)
@@ -477,17 +481,14 @@ def tile_randlorafullrankbasissum_x2_kernel(
         out_turn(4)
         out_turn(5)
         store(4, 6)
-        for term, j in LATE[2]:
-            stage2(term, j, False)
         vec(len(stream))
-        round_out(4, 6, False)
         plane_turn(0, 0)
-        turn_parts(6, False, True)
-        turn_parts(7, False, True)
+        round_out(4, 6, False)
+        mm_plane(0, 1)
         out_turn(6)
         out_turn(7, True)
         store(6, 8)
-        plane_turn(0, 1)
+        drain_plane(0, 1)
         round_out(6, 7)
         round_out(7, 8)
         plane_quant(0, 0)

@@ -22,15 +22,23 @@ KG = D // 512
 TT = TOK // P
 NJ = F // P
 X_RUNS = ((0, 2), (2, 4))
-V_SHARE = ((0, 64), (0, 48), (0, 32), (0, 40))
-BASE_AT = ((), (0,1), (2,3,4,5,6,7), ())
-EARLY = ((), (), ((0, 0),), ((0, 3),))
-MID = ((), (), (), ((0, 1), (0, 2)))
-LATE = (((0,4),(0,5)),((0,6),(0,7),(1,6),(1,7)),())
-BASE_MM = ((), (0,1,2,3), (4,5,6,7), ())
-AHEAD = 4
-ON_SCALAR = [unit for group in EARLY + MID + LATE for unit in group]
+V_SHARE = ((64, 40), (28, 32), (0, 48), (0, 48))
+BASE_AT = ((), (0,1,2), (3,4,5,6,7), ())
+EARLY = ((), (), (), ())
+MID = ((), (), (), ((0, 2), (0, 3)))
+LATE = ((0,4),(0,5),(1,4),(1,5),(0,6),(1,6),(0,7),(1,7))
+BASE_MM = ((0,1), (2,3,4), (5,6,7), ())
+AHEAD = 3
+ON_SCALAR = [unit for group in EARLY + MID + (LATE,) for unit in group]
 WALK = (1, 0)
+ON_POOL = ((2,1),(3,1))
+PLAIN = (0,) * 8
+RING = 4
+F_AT = 0
+SEEDED = 6
+ROUND_ON = (False,False,2)
+PLANE_AT = {-1: ((0, 0),)}
+OLD_AT = {-5: (6,), -1: (7,)}
 
 
 def tile_randlorafullrankbasissum_x2_kernel(
@@ -43,25 +51,27 @@ def tile_randlorafullrankbasissum_x2_kernel(
         ctx.enter_context(tc.manual_schedule())
 
         free_banks = list(range(8))
+        vector_ring = []
         bank_number = {}
 
         def sb(name, shape, dtype):
             return keep.tile(shape, dtype, name=name, align_bytes=64)
 
-        def new_bank(name, shape, dtype=F32):
-            number = free_banks.pop(0)
-            bank_number[name] = number
+        def new_bank(name, shape, dtype=F32, ring=free_banks):
+            number = ring.pop(0)
+            bank_number[name] = (number, ring)
             return psum.tile(shape, dtype, name=name, tag="bank%d" % number, bufs=1)
 
         def release(name):
-            free_banks.append(bank_number.pop(name))
+            number, ring = bank_number.pop(name)
+            ring.append(number)
 
         x_sb = [sb("x_sb%d" % i, [P, D], BF16) for i in range(TT)]
         xg = [sb("xg%d" % n, [P, KG, P * (i1 - i0), 4], BF16) for n, (i0, i1) in enumerate(X_RUNS)]
         xq = sb("xq", [P, KG, TOK], U32)
         xs = sb("xs", [P, KG, TOK], U8)
         braw = {(m, g): sb("braw%d_%d" % (m, g), [P, 4, R], BF16) for m in range(NB) for g in range(KG)}
-        bgr = [sb("bgr%d" % m, [P, KG, 4 * R], BF16) for m in range(NB)]
+        bgr = {}
         bq = [sb("bq%d" % m, [P, KG, R], U32) for m in range(NB)]
         bs = [sb("bs%d" % m, [P, KG, R], U8) for m in range(NB)]
         w0 = sb("w0", [P, KG, 2 * F], U8)
@@ -108,19 +118,28 @@ def tile_randlorafullrankbasissum_x2_kernel(
                 )
 
         def interleave(m, g, on_vector, c0, c1):
-            if c1 > c0:
+            if (m, g) not in bgr:
+                tag = "bgr_late" if g == 1 and m > 0 else "bgr%d_%d" % (m, g)
+                bgr[(m, g)] = keep.tile([P, 4 * R], BF16, name="bgr%d_%d" % (m, g), tag=tag, align_bytes=64)
+            if c1 > c0 and on_vector == 2:
+                dst = bgr[(m, g)][:].rearrange("p (t n j) -> p n t j", t=4, j=4)
+                src = braw[(m, g)][:].rearrange("p j (n t) -> p n t j", t=4)
+                nc.gpsimd.tensor_scalar(
+                    out=dst[:, 2 * c0 : 2 * c1], in0=src[:, 2 * c0 : 2 * c1], scalar1=1.0, scalar2=-0.0, op0=MULT, op1=ADD
+                )
+            elif c1 > c0:
                 copy = nc.vector.tensor_copy if on_vector else nc.scalar.copy
                 if WALK[on_vector] == 0:
-                    dst = bgr[m][:, g, :].rearrange("p (t c i j) -> p c t i j", t=4, i=2, j=4)
+                    dst = bgr[(m, g)][:].rearrange("p (t c i j) -> p c t i j", t=4, i=2, j=4)
                     src = braw[(m, g)][:].rearrange("p j (c i t) -> p c t i j", i=2, t=4)
                     copy(out=dst[:, c0:c1], in_=src[:, c0:c1])
                 else:
-                    dst = bgr[m][:, g, :].rearrange("p (t n j) -> p n j t", t=4, j=4)
+                    dst = bgr[(m, g)][:].rearrange("p (t n j) -> p n j t", t=4, j=4)
                     src = braw[(m, g)][:].rearrange("p j (n t) -> p n j t", t=4)
                     copy(out=dst[:, 2 * c0 : 2 * c1], in_=src[:, 2 * c0 : 2 * c1])
 
         def inter_v(m, g):
-            interleave(m, g, True, 0, V_SHARE[m][g])
+            interleave(m, g, 2 if (m, g) in ON_POOL else True, 0, V_SHARE[m][g])
 
         def inter_s(m, g, half=None):
             c0, c1 = V_SHARE[m][g], 64
@@ -138,7 +157,7 @@ def tile_randlorafullrankbasissum_x2_kernel(
             release("warm")
 
         def quant_b(m, g):
-            nc.vector.quantize_mx(out=bq[m][:, g, :].bitcast(FP8X4), scales=bs[m][:, g, :], in_=bgr[m][:, g, :])
+            nc.vector.quantize_mx(out=bq[m][:, g, :].bitcast(FP8X4), scales=bs[m][:, g, :], in_=bgr[(m, g)][:])
 
         def mm_x(i):
             words = x_sb[i][:].bitcast(F32)
@@ -171,7 +190,7 @@ def tile_randlorafullrankbasissum_x2_kernel(
             for u in range(2):
                 nc.tensor.transpose(bank[:, u, :], lam_rows[:, u : R // 2 : 2], ident[:])
             dst = lam_t[:].rearrange("p m o t -> p m (o t)").bitcast(F32)
-            nc.vector.tensor_copy(out=dst, in_=bank[:, :, 0:NB].rearrange("p u m -> p m u"))
+            nc.scalar.copy(out=dst, in_=bank[:, :, 0:NB].rearrange("p u m -> p m u"))
             release("lam_bank")
 
         def gam_turn():
@@ -234,8 +253,8 @@ def tile_randlorafullrankbasissum_x2_kernel(
             nc.scalar.copy(out=piece[:], in_=bank[:])
             parts[j].append(piece)
 
-        def mm_u(m, j):
-            bank = new_bank("u%d_%d" % (m, j), [P, TOK])
+        def mm_u(m, j, ring=free_banks):
+            bank = new_bank("u%d_%d" % (m, j), [P, TOK], F32, ring)
             held[("u", m, j)] = bank
             nc.tensor.matmul_mx(
                 out=bank[:],
@@ -265,14 +284,14 @@ def tile_randlorafullrankbasissum_x2_kernel(
 
         def pool_add(j, fresh=False):
             last = parts[j].pop()
-            acc = parts[j][0]
+            acc = parts[j][0 if j < SEEDED else 1]
             total = acc
             if fresh:
                 total = keep.tile([P, TOK], F32, name="sum%d" % j, tag="hl3", align_bytes=64)
                 parts[j][0] = total
             nc.gpsimd.tensor_tensor(out=total[:], in0=acc[:], in1=last[:], op=ADD)
 
-        def turn_parts(j, last, keep_first=False):
+        def turn_parts(j, last, keep_first=False, plain=0):
             first = j not in out_bank
             if first:
                 out_bank[j] = new_bank("o%d" % j, [P, TT, P])
@@ -288,7 +307,7 @@ def tile_randlorafullrankbasissum_x2_kernel(
                         rhs=ident[:],
                         start=(first and n == 0 and i == 0),
                         stop=(last and n == len(order) - 1 and i == TT - 1),
-                        is_transpose=True,
+                        is_transpose=(n > 0 or i >= plain),
                     )
 
         def drain_out(j, on_vector=False):
@@ -302,6 +321,11 @@ def tile_randlorafullrankbasissum_x2_kernel(
                 out=out_0[:, P * j0 : P * j1].rearrange("(i p) f -> p i f", p=P),
                 in_=o32[j0 // 2][:, :, P * (j0 % 2) : P * (j0 % 2 + j1 - j0)],
             )
+
+        def round_bank(j):
+            q0 = 32 * (j % 4)
+            dst = o16[j // 4][:].rearrange("p u i (q e) -> p u i q e", e=2)[:, :, :, q0 : q0 + 32, :]
+            nc.vector.tensor_copy(out=dst, in_=out_bank[j][:].rearrange("p i (q u e) -> p u i q e", u=2, e=2))
 
         def round_out(j0, j1, on_vector=True):
             q0 = 32 * (j0 % 4)
@@ -352,7 +376,7 @@ def tile_randlorafullrankbasissum_x2_kernel(
             drain_h(m, i)
 
         def stage2(m, j, on_vector):
-            mm_u(m, j)
+            mm_u(m, j, vector_ring if on_vector else free_banks)
             drain_u(m, j, on_vector)
 
         def base(j):
@@ -364,7 +388,7 @@ def tile_randlorafullrankbasissum_x2_kernel(
             drain_x(i)
 
         def out_turn(j, on_vector=False):
-            turn_parts(j, True)
+            turn_parts(j, True, False, PLAIN[j])
             drain_out(j, on_vector)
 
         def plane_turn(g, h, on_vector=False):
@@ -374,8 +398,8 @@ def tile_randlorafullrankbasissum_x2_kernel(
         nc.vector.memset(lam_rows[:], 0.0)
         nc.vector.memset(gam_rows[:], 0.0)
         make_identity(nc, ident[:])
-        nc.vector.memset(w0s[:].rearrange("p g n -> p (g n)").bitcast(I32), 0)
-        nc.vector.memset(aws[:].bitcast(I32), 0)
+        nc.gpsimd.memset(w0s[:].rearrange("p g n -> p (g n)").bitcast(I32), 0)
+        nc.gpsimd.memset(aws[:].bitcast(I32), 0)
         nc.scalar.dma_start(out=lam_rows[0:NB, :].bitcast(BF16), in_=lam[:, :])
         nc.scalar.dma_start(out=gam_rows[0 : NB * NJ, :], in_=gam.rearrange("m (j p) -> (m j) p", p=P))
         nc.scalar.activation(out=ident_b[:], in_=ident[:], func=COPY)
@@ -388,32 +412,31 @@ def tile_randlorafullrankbasissum_x2_kernel(
         load_b(1, 0)
         load_b(1, 1)
         load_b(2, 0)
-        load_b(2, 1)
         load_w0_scales()
         nc.sync.dma_start(out=w0[:].bitcast(I32), in_=w0_words.rearrange("g p b -> p g b").bitcast(I32))
+        load_b(2, 1)
         load_b(3, 0)
         load_b(3, 1)
         load_a_scales()
         nc.sync.dma_start(out=aw[:].bitcast(I32), in_=a_words[0].bitcast(I32))
 
-        lam_turn()
-        inter_s(0, 0)
         inter_v(0, 0)
-        x_turn(0)
-        inter_s(0, 1)
-        inter_v(0, 1)
+        inter_s(0, 0)
         quant_b(0, 0)
+        x_turn(0)
+        inter_v(0, 1)
+        inter_s(0, 1)
         quant_b(0, 1)
+        lam_turn()
         x_turn(1)
         quant_x(0)
         x_turn(2)
         x_turn(3)
+        gam_turn()
         inter_v(1, 0)
         inter_s(1, 0)
         inter_s(1, 1)
-        inter_v(1, 1)
         quant_x(1)
-        gam_turn()
 
         for m in range(NB):
             more = m + 1 < NB
@@ -424,11 +447,11 @@ def tile_randlorafullrankbasissum_x2_kernel(
             mm_h(m, 2)
             mm_h(m, 3)
             drain_h(m, 0)
+            drain_h(m, 1)
             if m > 0:
                 quant_h(m - 1)
-            if more and m > 0:
-                inter_v(m + 1, 1)
-            drain_h(m, 1)
+            else:
+                inter_v(1, 1)
             if more:
                 quant_b(m + 1, 0)
                 quant_b(m + 1, 1)
@@ -437,65 +460,57 @@ def tile_randlorafullrankbasissum_x2_kernel(
             for j in BASE_AT[m]:
                 drain_base(j)
             if m + 2 < NB:
+                if (m + 2, 1) in ON_POOL:
+                    inter_v(m + 2, 1)
                 inter_s(m + 2, 0)
                 inter_s(m + 2, 1)
             drain_h(m, 2)
             drain_h(m, 3)
+            if m + 2 < NB and (m + 2, 1) not in ON_POOL:
+                inter_v(m + 2, 1)
             for term, j in EARLY[m]:
                 stage2(term, j, False)
 
         stream = [(term, j + k) for j in range(0, NJ, 2) for term in range(NB) for k in range(2)]
         stream = [unit for unit in stream if unit not in ON_SCALAR]
-
-        def vec(n):
-            for k in range(n):
-                term, j = stream.pop(0)
-                stage2(term, j, True)
-
-        def upto(unit, more):
-            vec(stream.index(unit) + 1 + more)
-
-        vec(1)
-        quant_h(3)
-        pool_add(2, True)
-        pool_add(3)
-        vec(2)
-        for term, j in LATE[0]:
-            stage2(term, j, False)
-            pool_add(j)
-        upto((3, 1), 0)
-        for term, j in LATE[1]:
-            stage2(term, j, False)
-            pool_add(j)
-        vec(AHEAD)
-        out_turn(0)
-        out_turn(1)
-        store(0, 2)
-        upto((3, 3), AHEAD)
-        round_out(0, 2, False)
-        out_turn(2)
-        out_turn(3)
-        store(2, 4)
-        upto((3, 5), AHEAD)
-        round_out(2, 4, False)
-        out_turn(4)
-        out_turn(5)
-        store(4, 6)
-        vec(len(stream))
-        plane_turn(0, 0)
-        round_out(4, 6, False)
-        mm_plane(0, 1)
-        out_turn(6)
-        out_turn(7, True)
+        for k in range(RING):
+            vector_ring.append(free_banks.pop(0))
+        side = list(LATE)
+        for pos, (term, j) in enumerate(stream):
+            stage2(term, j, True)
+            if pos == F_AT:
+                quant_h(3)
+                pool_add(2, True)
+                pool_add(3)
+            if pos >= F_AT and side:
+                late, k = side.pop(0)
+                stage2(late, k, False)
+                if k < SEEDED or late == 1:
+                    pool_add(k)
+            ahead = AHEAD + 1 if pos == len(stream) - 1 else AHEAD
+            if pos >= ahead and stream[pos - ahead][0] == NB - 1 and pos != len(stream) - 2:
+                done = stream[pos - ahead][1]
+                if done < 6:
+                    out_turn(done)
+                if done % 2 == 1:
+                    store(done - 1, done + 1)
+                    round_out(done - 1, done + 1, ROUND_ON[done // 2])
+            for g, h in PLANE_AT.get(pos - len(stream), ()):
+                plane_turn(g, h)
+            for k in OLD_AT.get(pos - len(stream), ()):
+                turn_parts(k, False, True)
+        free_banks.extend(vector_ring)
+        for j in (6, 7):
+            turn_parts(j, True, False, PLAIN[j])
+            round_bank(j)
+            drain_out(j)
         store(6, 8)
-        drain_plane(0, 1)
-        round_out(6, 7)
-        round_out(7, 8)
+        plane_turn(0, 1)
         plane_quant(0, 0)
         plane_turn(1, 0)
+        plane_turn(1, 1, True)
         plane_quant(0, 1)
         plane_store(0)
-        plane_turn(1, 1, True)
         plane_quant(1, 0)
         plane_store(1, 0, 1)
         plane_quant(1, 1)

@@ -23,22 +23,20 @@ TT = TOK // P
 NJ = F // P
 X_RUNS = ((0, 2), (2, 4))
 V_SHARE = ((64, 40), (28, 32), (0, 48), (0, 48))
-BASE_AT = ((), (0,1,2), (3,4,5,6,7), ())
-EARLY = ((), (), (), ())
-MID = ((), (), (), ((0, 2), (0, 3)))
-LATE = ((0,4),(0,5),(1,4),(1,5),(0,6),(1,6),(0,7),(1,7))
-BASE_MM = ((0,1), (2,3,4), (5,6,7), ())
-AHEAD = 3
-ON_SCALAR = [unit for group in EARLY + MID + (LATE,) for unit in group]
 WALK = (1, 0)
-ON_POOL = ((2,1),(3,1))
+ON_POOL = ((2, 1), (3, 1))
 PLAIN = (0,) * 8
-RING = 4
-F_AT = 0
-SEEDED = 6
-ROUND_ON = (False,False,2)
-PLANE_AT = {-1: ((0, 0),)}
-OLD_AT = {-5: (6,), -1: (7,)}
+RING = 5
+SEEDED = 8
+ROUND_ON = (False, False, 2)
+MID = ((), (), (), (("drain", 4), (0, 4)))
+SIDE = ((), (("base", 0), ("base", 1), ("mm", 2), ("mm", 3)), (("drain", 2), (0, 2), ("drain", 3), (0, 3), ("mm", 4), ("mm", 5)), ())
+EARLY_ADDS = ((0, 2), (0, 3), (0, 4))
+LATE = ((1, 2), (1, 3), ("drain", 5), (0, 5), (1, 4), (1, 5), ("base", 6), ("base", 7), (0, 6), (0, 7), (1, 6))
+LATE_ADDS = ((1, 2), (1, 3), (0, 5), (1, 4), (1, 5), (0, 6), (0, 7), (1, 6))
+ON_SCALAR = [unit for group in MID + SIDE + (LATE,) for unit in group]
+PLANE_AT = {-1: ((0, 0), (0, 1))}
+TURN_AT = {11: (0, 1), 15: (2, 3), 18: (4, 5)}
 
 
 def tile_randlorafullrankbasissum_x2_kernel(
@@ -150,10 +148,10 @@ def tile_randlorafullrankbasissum_x2_kernel(
                 c0 = mid
             interleave(m, g, False, c0, c1)
 
-        def warm(n):
-            bank = new_bank("warm", [P, P])
+        def warm(n, moving):
+            bank = new_bank("warm", [P, moving.shape[1]])
             for k in range(n):
-                nc.tensor.matmul(bank[:], lhsT=ident[:], rhs=ident[:], start=True, stop=True)
+                nc.tensor.matmul(bank[:], lhsT=ident[:], rhs=moving, start=True, stop=True)
             release("warm")
 
         def quant_b(m, g):
@@ -282,12 +280,12 @@ def tile_randlorafullrankbasissum_x2_kernel(
                 nc.scalar.activation(out=piece[:], in_=bank[:], func=COPY, scale=col)
                 parts[j].append(piece)
 
-        def pool_add(j, fresh=False):
+        def pool_add(j, fresh=None):
             last = parts[j].pop()
             acc = parts[j][0 if j < SEEDED else 1]
             total = acc
             if fresh:
-                total = keep.tile([P, TOK], F32, name="sum%d" % j, tag="hl3", align_bytes=64)
+                total = keep.tile([P, TOK], F32, name="sum%d" % j, tag=fresh, align_bytes=64)
                 parts[j][0] = total
             nc.gpsimd.tensor_tensor(out=total[:], in0=acc[:], in1=last[:], op=ADD)
 
@@ -322,10 +320,33 @@ def tile_randlorafullrankbasissum_x2_kernel(
                 in_=o32[j0 // 2][:, :, P * (j0 % 2) : P * (j0 % 2 + j1 - j0)],
             )
 
-        def round_bank(j):
+        def round_bank(bank, j, i0, i1, copy):
             q0 = 32 * (j % 4)
-            dst = o16[j // 4][:].rearrange("p u i (q e) -> p u i q e", e=2)[:, :, :, q0 : q0 + 32, :]
-            nc.vector.tensor_copy(out=dst, in_=out_bank[j][:].rearrange("p i (q u e) -> p u i q e", u=2, e=2))
+            dst = o16[j // 4][:].rearrange("p u i (q e) -> p u i q e", e=2)[:, :, i0:i1, q0 : q0 + 32, :]
+            copy(out=dst, in_=bank[:].rearrange("p i (q u e) -> p u i q e", u=2, e=2))
+
+        def last_tiles():
+            turn_parts(6, True)
+            round_bank(out_bank[6], 6, 0, TT, nc.scalar.copy)
+            drain_out(6)
+            halves = []
+            for h in range(2):
+                bank = new_bank("o7_%d" % h, [P, 2, P])
+                halves.append(bank)
+                for ii in range(2):
+                    i = 2 * h + ii
+                    nc.tensor.transpose(bank[:, ii, :], parts[7][0][:, P * i : P * (i + 1)], ident[:])
+                round_bank(bank, 7, 2 * h, 2 * h + 2, nc.vector.tensor_copy)
+            for h in range(2):
+                nc.scalar.copy(out=o32[3][:, 2 * h : 2 * h + 2, P : 2 * P], in_=halves[h][:])
+                release("o7_%d" % h)
+
+        def store_last():
+            for h in range(2):
+                nc.sync.dma_start(
+                    out=out_0[256 * h : 256 * (h + 1), 6 * P : 8 * P].rearrange("(i p) f -> p i f", p=P),
+                    in_=o32[3][:, 2 * h : 2 * h + 2, :],
+                )
 
         def round_out(j0, j1, on_vector=True):
             q0 = 32 * (j0 % 4)
@@ -366,8 +387,7 @@ def tile_randlorafullrankbasissum_x2_kernel(
 
         def scale_store():
             for q in range(4):
-                eng = nc.sync if q % 2 == 0 else nc.scalar
-                eng.dma_start(
+                nc.scalar.dma_start(
                     out=out_2[:, 4 * q : 4 * q + 4, :].bitcast(I32), in_=ps[32 * q : 32 * q + 8, :].bitcast(I32)
                 )
 
@@ -395,6 +415,11 @@ def tile_randlorafullrankbasissum_x2_kernel(
             mm_plane(g, h)
             drain_plane(g, h, on_vector)
 
+        def out_last(j):
+            turn_parts(j, True)
+            round_bank(out_bank[j], j, 0, TT, nc.vector.tensor_copy)
+            drain_out(j)
+
         nc.vector.memset(lam_rows[:], 0.0)
         nc.vector.memset(gam_rows[:], 0.0)
         make_identity(nc, ident[:])
@@ -412,16 +437,16 @@ def tile_randlorafullrankbasissum_x2_kernel(
         load_b(1, 0)
         load_b(1, 1)
         load_b(2, 0)
+        load_b(2, 1)
         load_w0_scales()
         nc.sync.dma_start(out=w0[:].bitcast(I32), in_=w0_words.rearrange("g p b -> p g b").bitcast(I32))
-        load_b(2, 1)
         load_b(3, 0)
         load_b(3, 1)
         load_a_scales()
         nc.sync.dma_start(out=aw[:].bitcast(I32), in_=a_words[0].bitcast(I32))
 
-        inter_v(0, 0)
         inter_s(0, 0)
+        inter_v(0, 0)
         quant_b(0, 0)
         x_turn(0)
         inter_v(0, 1)
@@ -438,81 +463,75 @@ def tile_randlorafullrankbasissum_x2_kernel(
         inter_s(1, 1)
         quant_x(1)
 
+        def side_work(steps):
+            for kind, j in steps:
+                if kind == "mm":
+                    mm_base(j)
+                elif kind == "drain":
+                    drain_base(j)
+                elif kind == "base":
+                    base(j)
+                else:
+                    stage2(kind, j, False)
+                    if (kind, j) in EARLY_ADDS:
+                        pool_add(j, "bgr_late" if (kind, j) == EARLY_ADDS[0] else None)
+
         for m in range(NB):
             more = m + 1 < NB
             mm_h(m, 0)
             mm_h(m, 1)
-            for term, j in MID[m]:
-                stage2(term, j, False)
+            side_work(MID[m])
             mm_h(m, 2)
             mm_h(m, 3)
             drain_h(m, 0)
             drain_h(m, 1)
-            if m > 0:
-                quant_h(m - 1)
-            else:
+            if m == 0:
                 inter_v(1, 1)
+            elif more:
+                quant_h(m - 1)
             if more:
                 quant_b(m + 1, 0)
                 quant_b(m + 1, 1)
-            for j in BASE_MM[m]:
-                mm_base(j)
-            for j in BASE_AT[m]:
-                drain_base(j)
+            side_work(SIDE[m])
             if m + 2 < NB:
-                if (m + 2, 1) in ON_POOL:
-                    inter_v(m + 2, 1)
+                inter_v(m + 2, 1)
                 inter_s(m + 2, 0)
                 inter_s(m + 2, 1)
             drain_h(m, 2)
             drain_h(m, 3)
-            if m + 2 < NB and (m + 2, 1) not in ON_POOL:
-                inter_v(m + 2, 1)
-            for term, j in EARLY[m]:
-                stage2(term, j, False)
 
         stream = [(term, j + k) for j in range(0, NJ, 2) for term in range(NB) for k in range(2)]
         stream = [unit for unit in stream if unit not in ON_SCALAR]
         for k in range(RING):
             vector_ring.append(free_banks.pop(0))
         side = list(LATE)
+        adds = list(LATE_ADDS)
         for pos, (term, j) in enumerate(stream):
             stage2(term, j, True)
-            if pos == F_AT:
+            if pos == 0:
+                quant_h(2)
                 quant_h(3)
-                pool_add(2, True)
-                pool_add(3)
-            if pos >= F_AT and side:
-                late, k = side.pop(0)
-                stage2(late, k, False)
-                if k < SEEDED or late == 1:
-                    pool_add(k)
-            ahead = AHEAD + 1 if pos == len(stream) - 1 else AHEAD
-            if pos >= ahead and stream[pos - ahead][0] == NB - 1 and pos != len(stream) - 2:
-                done = stream[pos - ahead][1]
-                if done < 6:
-                    out_turn(done)
-                if done % 2 == 1:
-                    store(done - 1, done + 1)
-                    round_out(done - 1, done + 1, ROUND_ON[done // 2])
+            if side:
+                side_work([side.pop(0)])
+            while adds and adds[0] not in side:
+                pool_add(adds[0][1], "hl3" if len(adds) == len(LATE_ADDS) else None)
+                adds.pop(0)
+            for k in TURN_AT.get(pos, ()):
+                out_turn(k)
+                if k % 2 == 1:
+                    store(k - 1, k + 1)
+                    round_out(k - 1, k + 1, ROUND_ON[k // 2])
             for g, h in PLANE_AT.get(pos - len(stream), ()):
                 plane_turn(g, h)
-            for k in OLD_AT.get(pos - len(stream), ()):
-                turn_parts(k, False, True)
         free_banks.extend(vector_ring)
-        for j in (6, 7):
-            turn_parts(j, True, False, PLAIN[j])
-            round_bank(j)
-            drain_out(j)
-        store(6, 8)
-        plane_turn(0, 1)
         plane_quant(0, 0)
-        plane_turn(1, 0)
-        plane_turn(1, 1, True)
+        last_tiles()
         plane_quant(0, 1)
         plane_store(0)
+        store_last()
+        plane_turn(1, 0, True)
+        plane_turn(1, 1)
         plane_quant(1, 0)
-        plane_store(1, 0, 1)
         plane_quant(1, 1)
-        plane_store(1, 1, 2)
+        plane_store(1)
         scale_store()

@@ -22,21 +22,22 @@ KG = D // 512
 TT = TOK // P
 NJ = F // P
 X_RUNS = ((0, 2), (2, 4))
-V_SHARE = ((64, 40), (28, 32), (0, 48), (0, 48))
+V_SHARE = ((40, 44), (64, 0), (0, 56), (0, 56))
 WALK = (1, 0)
 ON_POOL = ((2, 1), (3, 1))
 PLAIN = (0,) * 8
 RING = 5
 SEEDED = 8
-ROUND_ON = (False, False, 2)
-MID = ((), (), (), (("drain", 4), (0, 4)))
-SIDE = ((), (("base", 0), ("base", 1), ("mm", 2), ("mm", 3)), (("drain", 2), (0, 2), ("drain", 3), (0, 3), ("mm", 4), ("mm", 5)), ())
+ROUND_ON = (False, 2, 2)
+MID = ((), (("base", 0), ("base", 1)), (("drain", 2), ("drain", 3), ("base", 4)), (("drain", 5), (0, 4), ("drain", 6)))
+SIDE = ((), (("mm", 2), ("mm", 3)), ((0, 2), (0, 3), ("mm", 5), ("mm", 6)), ())
 EARLY_ADDS = ((0, 2), (0, 3), (0, 4))
-LATE = ((1, 2), (1, 3), ("drain", 5), (0, 5), (1, 4), (1, 5), ("base", 6), ("base", 7), (0, 6), (0, 7), (1, 6))
-LATE_ADDS = ((1, 2), (1, 3), (0, 5), (1, 4), (1, 5), (0, 6), (0, 7), (1, 6))
+LATE = ((1, 2), (1, 3), (0, 5), (1, 4), (1, 5), ("base", 7), (0, 6), (0, 7))
+LATE_ADDS = ((1, 2), (1, 3), (0, 5), (1, 4), (1, 5), (0, 6), (0, 7))
 ON_SCALAR = [unit for group in MID + SIDE + (LATE,) for unit in group]
 PLANE_AT = {-1: ((0, 0), (0, 1))}
 TURN_AT = {11: (0, 1), 15: (2, 3), 18: (4, 5)}
+LAST_V = True
 
 
 def tile_randlorafullrankbasissum_x2_kernel(
@@ -139,6 +140,9 @@ def tile_randlorafullrankbasissum_x2_kernel(
         def inter_v(m, g):
             interleave(m, g, 2 if (m, g) in ON_POOL else True, 0, V_SHARE[m][g])
 
+        def inter_rest(m, g):
+            interleave(m, g, True, V_SHARE[m][g], 64)
+
         def inter_s(m, g, half=None):
             c0, c1 = V_SHARE[m][g], 64
             mid = (c0 + c1) // 2
@@ -188,13 +192,13 @@ def tile_randlorafullrankbasissum_x2_kernel(
             for u in range(2):
                 nc.tensor.transpose(bank[:, u, :], lam_rows[:, u : R // 2 : 2], ident[:])
             dst = lam_t[:].rearrange("p m o t -> p m (o t)").bitcast(F32)
-            nc.scalar.copy(out=dst, in_=bank[:, :, 0:NB].rearrange("p u m -> p m u"))
+            nc.vector.tensor_copy(out=dst, in_=bank[:, :, 0:NB].rearrange("p u m -> p m u"))
             release("lam_bank")
 
         def gam_turn():
             bank = new_bank("gam_bank", [P, P], BF16)
             nc.tensor.transpose(bank[:], gam_rows[:], ident_b[:])
-            nc.scalar.copy(out=gam_t[:], in_=bank[:, 0 : NB * NJ])
+            nc.vector.tensor_copy(out=gam_t[:], in_=bank[:, 0 : NB * NJ])
             release("gam_bank")
 
         def mm_h(m, i):
@@ -327,7 +331,7 @@ def tile_randlorafullrankbasissum_x2_kernel(
 
         def last_tiles():
             turn_parts(6, True)
-            round_bank(out_bank[6], 6, 0, TT, nc.scalar.copy)
+            round_bank(out_bank[6], 6, 0, TT, nc.vector.tensor_copy if LAST_V else nc.scalar.copy)
             drain_out(6)
             halves = []
             for h in range(2):
@@ -452,12 +456,12 @@ def tile_randlorafullrankbasissum_x2_kernel(
         inter_v(0, 1)
         inter_s(0, 1)
         quant_b(0, 1)
-        lam_turn()
         x_turn(1)
+        lam_turn()
+        gam_turn()
         quant_x(0)
         x_turn(2)
         x_turn(3)
-        gam_turn()
         inter_v(1, 0)
         inter_s(1, 0)
         inter_s(1, 1)
@@ -488,6 +492,7 @@ def tile_randlorafullrankbasissum_x2_kernel(
             if m == 0:
                 inter_v(1, 1)
             elif more:
+                inter_rest(m + 1, 1)
                 quant_h(m - 1)
             if more:
                 quant_b(m + 1, 0)
@@ -496,7 +501,6 @@ def tile_randlorafullrankbasissum_x2_kernel(
             if m + 2 < NB:
                 inter_v(m + 2, 1)
                 inter_s(m + 2, 0)
-                inter_s(m + 2, 1)
             drain_h(m, 2)
             drain_h(m, 3)
 
@@ -525,10 +529,13 @@ def tile_randlorafullrankbasissum_x2_kernel(
                 plane_turn(g, h)
         free_banks.extend(vector_ring)
         plane_quant(0, 0)
-        last_tiles()
+        plane_store(0, 0, 1)
+        out_last(6)
+        store(6, 7)
+        out_last(7)
         plane_quant(0, 1)
-        plane_store(0)
-        store_last()
+        plane_store(0, 1, 2)
+        store(7, 8)
         plane_turn(1, 0, True)
         plane_turn(1, 1)
         plane_quant(1, 0)

@@ -21,23 +21,13 @@ P = 128
 KG = D // 512
 TT = TOK // P
 NJ = F // P
-X_RUNS = ((0, 2), (2, 4))
-V_SHARE = ((40, 44), (64, 0), (0, 56), (0, 56))
-WALK = (1, 0)
-ON_POOL = ((2, 1), (3, 1))
-PLAIN = (0,) * 8
-RING = 5
-SEEDED = 8
-ROUND_ON = (False, 2, 2)
-MID = ((), (("base", 0), ("base", 1)), (("drain", 2), ("drain", 3), ("base", 4)), (("drain", 5), (0, 4), ("drain", 6)))
-SIDE = ((), (("mm", 2), ("mm", 3)), ((0, 2), (0, 3), ("mm", 5), ("mm", 6)), ())
-EARLY_ADDS = ((0, 2), (0, 3), (0, 4))
-LATE = ((1, 2), (1, 3), (0, 5), (1, 4), (1, 5), ("base", 7), (0, 6), (0, 7))
-LATE_ADDS = ((1, 2), (1, 3), (0, 5), (1, 4), (1, 5), (0, 6), (0, 7))
-ON_SCALAR = [unit for group in MID + SIDE + (LATE,) for unit in group]
-PLANE_AT = {-1: ((0, 0), (0, 1))}
-TURN_AT = {11: (0, 1), 15: (2, 3), 18: (4, 5)}
-LAST_V = True
+PIECES = R // 8
+
+HELPER_PIECES = {(0, 0): 40, (0, 1): 40, (1, 0): 24, (1, 1): 24, (2, 0): 0, (2, 1): 44, (3, 0): 0, (3, 1): 44}
+FIRST_SHARED = 2
+FIRST_TWO_PARTS = 6
+VECTOR_BANKS = 4
+AHEAD = 3
 
 
 def tile_randlorafullrankbasissum_x2_kernel(
@@ -49,496 +39,378 @@ def tile_randlorafullrankbasissum_x2_kernel(
         psum = ctx.enter_context(tc.psum_pool(name="psum", bufs=1))
         ctx.enter_context(tc.manual_schedule())
 
+        def sb(name, shape, dtype, tag=None):
+            return keep.tile(shape, dtype, name=name, tag=tag or name, align_bytes=64)
+
         free_banks = list(range(8))
         vector_ring = []
-        bank_number = {}
+        in_use = {}
 
-        def sb(name, shape, dtype):
-            return keep.tile(shape, dtype, name=name, align_bytes=64)
-
-        def new_bank(name, shape, dtype=F32, ring=free_banks):
+        def take_bank(name, shape, dtype=F32, ring=free_banks):
             number = ring.pop(0)
-            bank_number[name] = (number, ring)
-            return psum.tile(shape, dtype, name=name, tag="bank%d" % number, bufs=1)
+            bank = psum.tile(shape, dtype, name=name, tag="bank%d" % number)
+            in_use[name] = (bank, number, ring)
+            return bank
 
-        def release(name):
-            number, ring = bank_number.pop(name)
+        def give_back(name):
+            bank, number, ring = in_use.pop(name)
             ring.append(number)
+            return bank
 
-        x_sb = [sb("x_sb%d" % i, [P, D], BF16) for i in range(TT)]
-        xg = [sb("xg%d" % n, [P, KG, P * (i1 - i0), 4], BF16) for n, (i0, i1) in enumerate(X_RUNS)]
-        xq = sb("xq", [P, KG, TOK], U32)
-        xs = sb("xs", [P, KG, TOK], U8)
-        braw = {(m, g): sb("braw%d_%d" % (m, g), [P, 4, R], BF16) for m in range(NB) for g in range(KG)}
-        bgr = {}
-        bq = [sb("bq%d" % m, [P, KG, R], U32) for m in range(NB)]
-        bs = [sb("bs%d" % m, [P, KG, R], U8) for m in range(NB)]
-        w0 = sb("w0", [P, KG, 2 * F], U8)
-        aw = sb("aw", [P, 2 * F], U8)
-        w0s = sb("w0s", [P, KG, F], U8)
-        aws = sb("aws", [P, F], U8)
-        gam_rows = sb("gam_rows", [P, P], BF16)
+        x_rows = [sb("x_rows%d" % i, [P, D], BF16) for i in range(TT)]
+        x_words = [sb("x_words%d" % h, [P, KG, 2 * P, 4], BF16) for h in range(2)]
+        x_codes = sb("x_codes", [P, KG, TOK], U32)
+        x_scales = sb("x_scales", [P, KG, TOK], U8)
+        b_rows = {(m, g): sb("b_rows%d_%d" % (m, g), [P, 4, R], BF16) for m in range(NB) for g in range(KG)}
+        b_words = {}
+        b_codes = [sb("b_codes%d" % m, [P, KG, R], U32) for m in range(NB)]
+        b_scales = [sb("b_scales%d" % m, [P, KG, R], U8) for m in range(NB)]
+        w0_codes = sb("w0_codes", [P, KG, 2 * F], U8)
+        w0_plane = sb("w0_plane", [P, KG, F], U8)
+        a_codes = sb("a_codes", [P, 2 * F], U8)
+        a_plane = sb("a_plane", [P, F], U8)
         lam_rows = sb("lam_rows", [P, R // 2], F32)
-        ident = sb("ident", [P, P], F32)
-        ident_b = sb("ident_b", [P, P], BF16)
+        gam_rows = sb("gam_rows", [P, P], BF16)
         lam_t = sb("lam_t", [P, NB, 1, 4], BF16)
         gam_t = sb("gam_t", [P, NB * NJ], F32)
+        ident = sb("ident", [P, P], F32)
+        ident_b = sb("ident_b", [P, P], BF16)
         hl = [sb("hl%d" % m, [P, TOK, 4], BF16) for m in range(NB)]
-        hq = [sb("hq%d" % m, [P, TOK], U32) for m in range(NB)]
-        hs = [sb("hs%d" % m, [P, TOK], U8) for m in range(NB)]
-        o32 = [sb("o32_%d" % jp, [P, TT, 2 * P], F32) for jp in range(NJ // 2)]
-        o16 = [sb("o16_%d" % g, [P, 2, TT, 256], BF16) for g in range(2)]
-        pg = {(g, h): sb("pg%d_%d" % (g, h), [P, 256, 4], BF16) for g in range(2) for h in range(2)}
-        pq = [sb("pq%d" % g, [P, TOK], U32) for g in range(2)]
-        ps = sb("ps", [P, TOK], U8)
+        hl_codes = [sb("hl_codes%d" % m, [P, TOK], U32) for m in range(NB)]
+        hl_scales = [sb("hl_scales%d" % m, [P, TOK], U8) for m in range(NB)]
         parts = [[] for j in range(NJ)]
-        out_bank = {}
-        held = {}
+        out32 = [sb("out32_%d" % pair, [P, TT, 2 * P], F32) for pair in range(NJ // 2)]
+        out16 = [sb("out16_%d" % g, [P, 2, TT, 2 * P], BF16) for g in range(2)]
+        p_words = {(g, h): sb("p_words%d_%d" % (g, h), [P, 2 * P, 4], BF16) for g in range(2) for h in range(2)}
+        p_codes = [sb("p_codes%d" % g, [P, TOK], U32) for g in range(2)]
+        p_plane = sb("p_plane", [P, TOK], U8)
 
         def load_x(i):
-            nc.sync.dma_start(out=x_sb[i][:], in_=x[P * i : P * (i + 1), :])
+            nc.sync.dma_start(out=x_rows[i][:], in_=x[P * i : P * (i + 1), :])
 
-        def load_b(m, g):
+        def load_basis(m, g):
             nc.sync.dma_start(
-                out=braw[(m, g)][:], in_=bases[m, 512 * g : 512 * (g + 1), :].rearrange("(p j) r -> p j r", j=4)
+                out=b_rows[(m, g)][:], in_=bases[m, 512 * g : 512 * (g + 1), :].rearrange("(p j) r -> p j r", j=4)
             )
 
-        def load_w0_scales():
-            for q in range(4):
-                nc.sync.dma_start(
-                    out=w0s[32 * q : 32 * q + 4, :, :].bitcast(I32),
-                    in_=w0_scales[:, 4 * q : 4 * q + 4, :].rearrange("g q n -> q g n").bitcast(I32),
-                )
+        nc.vector.memset(lam_rows[:], 0.0)
+        nc.vector.memset(gam_rows[:], 0.0)
+        make_identity(nc, ident[:])
+        nc.gpsimd.memset(w0_plane[:].rearrange("p g n -> p (g n)").bitcast(I32), 0)
+        nc.gpsimd.memset(a_plane[:].bitcast(I32), 0)
+        nc.scalar.dma_start(out=lam_rows[0:NB, :].bitcast(BF16), in_=lam[:, :])
+        nc.scalar.dma_start(out=gam_rows[0 : NB * NJ, :], in_=gam.rearrange("m (j p) -> (m j) p", p=P))
+        nc.scalar.activation(out=ident_b[:], in_=ident[:], func=COPY)
 
-        def load_a_scales():
-            for q in range(4):
-                nc.sync.dma_start(
-                    out=aws[32 * q : 32 * q + 4, :].bitcast(I32), in_=a_scales[0, 4 * q : 4 * q + 4, :].bitcast(I32)
-                )
+        load_basis(0, 0)
+        load_x(0)
+        load_basis(0, 1)
+        for i in range(1, TT):
+            load_x(i)
+        for m in (1, 2):
+            for g in range(KG):
+                load_basis(m, g)
+        for q in range(4):
+            nc.sync.dma_start(
+                out=w0_plane[32 * q : 32 * q + 4, :, :].bitcast(I32),
+                in_=w0_scales[:, 4 * q : 4 * q + 4, :].rearrange("g q n -> q g n").bitcast(I32),
+            )
+        nc.sync.dma_start(out=w0_codes[:].bitcast(I32), in_=w0_words.rearrange("g p b -> p g b").bitcast(I32))
+        for g in range(KG):
+            load_basis(3, g)
+        for q in range(4):
+            nc.sync.dma_start(
+                out=a_plane[32 * q : 32 * q + 4, :].bitcast(I32), in_=a_scales[0, 4 * q : 4 * q + 4, :].bitcast(I32)
+            )
+        nc.sync.dma_start(out=a_codes[:].bitcast(I32), in_=a_words[0].bitcast(I32))
 
-        def interleave(m, g, on_vector, c0, c1):
-            if (m, g) not in bgr:
-                tag = "bgr_late" if g == 1 and m > 0 else "bgr%d_%d" % (m, g)
-                bgr[(m, g)] = keep.tile([P, 4 * R], BF16, name="bgr%d_%d" % (m, g), tag=tag, align_bytes=64)
-            if c1 > c0 and on_vector == 2:
-                dst = bgr[(m, g)][:].rearrange("p (t n j) -> p n t j", t=4, j=4)
-                src = braw[(m, g)][:].rearrange("p j (n t) -> p n t j", t=4)
-                nc.gpsimd.tensor_scalar(
-                    out=dst[:, 2 * c0 : 2 * c1], in0=src[:, 2 * c0 : 2 * c1], scalar1=1.0, scalar2=-0.0, op0=MULT, op1=ADD
-                )
-            elif c1 > c0:
-                copy = nc.vector.tensor_copy if on_vector else nc.scalar.copy
-                if WALK[on_vector] == 0:
-                    dst = bgr[(m, g)][:].rearrange("p (t c i j) -> p c t i j", t=4, i=2, j=4)
-                    src = braw[(m, g)][:].rearrange("p j (c i t) -> p c t i j", i=2, t=4)
-                    copy(out=dst[:, c0:c1], in_=src[:, c0:c1])
-                else:
-                    dst = bgr[(m, g)][:].rearrange("p (t n j) -> p n j t", t=4, j=4)
-                    src = braw[(m, g)][:].rearrange("p j (n t) -> p n j t", t=4)
-                    copy(out=dst[:, 2 * c0 : 2 * c1], in_=src[:, 2 * c0 : 2 * c1])
+        def interleave_views(m, g, walk, first, last):
+            if (m, g) not in b_words:
+                tag = "b_words_second" if g == 1 and m > 0 else None
+                b_words[(m, g)] = sb("b_words%d_%d" % (m, g), [P, 4 * R], BF16, tag)
+            dst = b_words[(m, g)][:].rearrange("p (t c i j) -> p " + walk, t=4, i=2, j=4)
+            src = b_rows[(m, g)][:].rearrange("p j (c i t) -> p " + walk, i=2, t=4)
+            step = dst.shape[1] // PIECES
+            return dst[:, step * first : step * last], src[:, step * first : step * last]
 
-        def inter_v(m, g):
-            interleave(m, g, 2 if (m, g) in ON_POOL else True, 0, V_SHARE[m][g])
+        def interleave_helper(m, g):
+            if m < 2:
+                dst, src = interleave_views(m, g, "c t i j", 0, HELPER_PIECES[(m, g)])
+                nc.vector.tensor_copy(out=dst, in_=src)
+            else:
+                dst, src = interleave_views(m, g, "(c i) t j", 0, HELPER_PIECES[(m, g)])
+                nc.gpsimd.tensor_scalar(out=dst, in0=src, scalar1=1.0, scalar2=-0.0, op0=MULT, op1=ADD)
 
-        def inter_rest(m, g):
-            interleave(m, g, True, V_SHARE[m][g], 64)
+        def interleave_scalar(m, g):
+            dst, src = interleave_views(m, g, "(c i) j t", HELPER_PIECES[(m, g)], PIECES)
+            nc.scalar.copy(out=dst, in_=src)
 
-        def inter_s(m, g, half=None):
-            c0, c1 = V_SHARE[m][g], 64
-            mid = (c0 + c1) // 2
-            if half == 0:
-                c1 = mid
-            if half == 1:
-                c0 = mid
-            interleave(m, g, False, c0, c1)
+        def quantise_basis(m, g):
+            nc.vector.quantize_mx(
+                out=b_codes[m][:, g, :].bitcast(FP8X4), scales=b_scales[m][:, g, :], in_=b_words[(m, g)][:]
+            )
 
-        def warm(n, moving):
-            bank = new_bank("warm", [P, moving.shape[1]])
-            for k in range(n):
-                nc.tensor.matmul(bank[:], lhsT=ident[:], rhs=moving, start=True, stop=True)
-            release("warm")
-
-        def quant_b(m, g):
-            nc.vector.quantize_mx(out=bq[m][:, g, :].bitcast(FP8X4), scales=bs[m][:, g, :], in_=bgr[(m, g)][:])
-
-        def mm_x(i):
-            words = x_sb[i][:].bitcast(F32)
-            bank = new_bank("xt%d" % i, [P, KG, 2, P])
-            held[("x", i)] = bank
+        def turn_x(i):
+            words = x_rows[i][:].bitcast(F32)
+            bank = take_bank("x%d" % i, [P, KG, 2, P])
             for g in range(KG):
                 for u in range(2):
                     nc.tensor.transpose(bank[:, g, u, :], words[:, 256 * g + u : 256 * (g + 1) : 2], ident[:])
+            give_back("x%d" % i)
+            dst = x_words[i // 2][:, :, P * (i % 2) : P * (i % 2 + 1), :].rearrange("p g n t -> p g (n t)").bitcast(F32)
+            nc.scalar.copy(
+                out=dst.rearrange("p g (n u) -> p g n u", u=2), in_=bank[:].rearrange("p g u n -> p g n u")
+            )
 
-        def drain_x(i):
-            bank = held.pop(("x", i))
-            release("xt%d" % i)
-            n = [n for n, (i0, i1) in enumerate(X_RUNS) if i0 <= i < i1][0]
-            sl = slice(P * (i - X_RUNS[n][0]), P * (i - X_RUNS[n][0] + 1))
-            dst = xg[n][:, :, sl, :].rearrange("p g n t -> p g (n t)").bitcast(F32)
-            dst = dst.rearrange("p g (n u) -> p g n u", u=2)
-            nc.scalar.copy(out=dst, in_=bank[:].rearrange("p g u n -> p g n u"))
-
-        def quant_x(h):
-            sl = slice(P * X_RUNS[h][0], P * X_RUNS[h][1])
+        def quantise_x(h):
+            tokens = slice(2 * P * h, 2 * P * (h + 1))
             for g in range(KG):
                 nc.vector.quantize_mx(
-                    out=xq[:, g, sl].bitcast(FP8X4),
-                    scales=xs[:, g, sl],
-                    in_=xg[h][:, g, :, :].rearrange("p n t -> p (n t)"),
+                    out=x_codes[:, g, tokens].bitcast(FP8X4),
+                    scales=x_scales[:, g, tokens],
+                    in_=x_words[h][:, g, :, :].rearrange("p n t -> p (n t)"),
                 )
 
-        def lam_turn():
-            bank = new_bank("lam_bank", [P, 2, P])
+        def turn_lam_and_gam():
+            bank = take_bank("lam", [P, 2, P])
             for u in range(2):
                 nc.tensor.transpose(bank[:, u, :], lam_rows[:, u : R // 2 : 2], ident[:])
-            dst = lam_t[:].rearrange("p m o t -> p m (o t)").bitcast(F32)
-            nc.vector.tensor_copy(out=dst, in_=bank[:, :, 0:NB].rearrange("p u m -> p m u"))
-            release("lam_bank")
-
-        def gam_turn():
-            bank = new_bank("gam_bank", [P, P], BF16)
+            nc.vector.tensor_copy(
+                out=lam_t[:].rearrange("p m o t -> p m (o t)").bitcast(F32),
+                in_=give_back("lam")[:, :, 0:NB].rearrange("p u m -> p m u"),
+            )
+            bank = take_bank("gam", [P, P], BF16)
             nc.tensor.transpose(bank[:], gam_rows[:], ident_b[:])
-            nc.vector.tensor_copy(out=gam_t[:], in_=bank[:, 0 : NB * NJ])
-            release("gam_bank")
+            nc.vector.tensor_copy(out=gam_t[:], in_=give_back("gam")[:, 0 : NB * NJ])
 
-        def mm_h(m, i):
-            bank = new_bank("h%d_%d" % (m, i), [P, 4, P])
-            held[("h", m, i)] = bank
-            sl = slice(P * i, P * (i + 1))
+        def multiply_h(m, i):
+            bank = take_bank("h%d_%d" % (m, i), [P, 4, P])
+            tokens = slice(P * i, P * (i + 1))
             for t in range(4):
                 cols = slice(P * t, P * (t + 1))
                 for g in range(KG):
                     nc.tensor.matmul_mx(
                         out=bank[:, t, :],
-                        lhsT=bq[m][:, g, cols].bitcast(FP8X4),
-                        lhsT_scale=bs[m][:, g, cols],
-                        rhs=xq[:, g, sl].bitcast(FP8X4),
-                        rhs_scale=xs[:, g, sl],
+                        lhsT=b_codes[m][:, g, cols].bitcast(FP8X4),
+                        lhsT_scale=b_scales[m][:, g, cols],
+                        rhs=x_codes[:, g, tokens].bitcast(FP8X4),
+                        rhs_scale=x_scales[:, g, tokens],
                         start=(g == 0),
                         stop=(g == KG - 1),
                     )
 
         def drain_h(m, i):
-            bank = held.pop(("h", m, i))
-            release("h%d_%d" % (m, i))
-            sl = slice(P * i, P * (i + 1))
             nc.vector.tensor_tensor(
-                out=hl[m][:, sl, :],
-                in0=bank[:].rearrange("p t n -> p n t"),
+                out=hl[m][:, P * i : P * (i + 1), :],
+                in0=give_back("h%d_%d" % (m, i))[:].rearrange("p t n -> p n t"),
                 in1=lam_t[:, m, :, :].to_broadcast([P, P, 4]),
                 op=MULT,
             )
 
-        def quant_h(m):
+        def quantise_hl(m):
             nc.vector.quantize_mx(
-                out=hq[m][:].bitcast(FP8X4), scales=hs[m][:], in_=hl[m][:].rearrange("p n t -> p (n t)")
+                out=hl_codes[m][:].bitcast(FP8X4), scales=hl_scales[m][:], in_=hl[m][:].rearrange("p n t -> p (n t)")
             )
 
-        def mm_base(j):
-            bank = new_bank("base%d" % j, [P, TOK])
-            held[("base", j)] = bank
+        def multiply_base(j):
+            bank = take_bank("base%d" % j, [P, TOK])
             for g in range(KG):
                 nc.tensor.matmul_mx(
                     out=bank[:],
-                    lhsT=w0[:, g, 256 * j : 256 * (j + 1)].bitcast(FP4X4),
-                    lhsT_scale=w0s[:, g, P * j : P * (j + 1)],
-                    rhs=xq[:, g, :].bitcast(FP8X4),
-                    rhs_scale=xs[:, g, :],
+                    lhsT=w0_codes[:, g, 2 * P * j : 2 * P * (j + 1)].bitcast(FP4X4),
+                    lhsT_scale=w0_plane[:, g, P * j : P * (j + 1)],
+                    rhs=x_codes[:, g, :].bitcast(FP8X4),
+                    rhs_scale=x_scales[:, g, :],
                     start=(g == 0),
                     stop=(g == KG - 1),
                 )
 
         def drain_base(j):
-            bank = held.pop(("base", j))
-            release("base%d" % j)
-            piece = sb("part_base%d" % j, [P, TOK], F32)
-            nc.scalar.copy(out=piece[:], in_=bank[:])
-            parts[j].append(piece)
+            part = sb("base_part%d" % j, [P, TOK], F32)
+            nc.scalar.copy(out=part[:], in_=give_back("base%d" % j)[:])
+            parts[j].append(part)
 
-        def mm_u(m, j, ring=free_banks):
-            bank = new_bank("u%d_%d" % (m, j), [P, TOK], F32, ring)
-            held[("u", m, j)] = bank
+        def multiply_u(m, j, ring):
+            bank = take_bank("u%d_%d" % (m, j), [P, TOK], F32, ring)
             nc.tensor.matmul_mx(
                 out=bank[:],
-                lhsT=aw[:, 256 * j : 256 * (j + 1)].bitcast(FP4X4),
-                lhsT_scale=aws[:, P * j : P * (j + 1)],
-                rhs=hq[m][:].bitcast(FP8X4),
-                rhs_scale=hs[m][:],
+                lhsT=a_codes[:, 2 * P * j : 2 * P * (j + 1)].bitcast(FP4X4),
+                lhsT_scale=a_plane[:, P * j : P * (j + 1)],
+                rhs=hl_codes[m][:].bitcast(FP8X4),
+                rhs_scale=hl_scales[m][:],
                 start=True,
                 stop=True,
             )
+            return give_back("u%d_%d" % (m, j)), gam_t[:, NJ * m + j : NJ * m + j + 1]
 
-        def drain_u(m, j, on_vector):
-            bank = held.pop(("u", m, j))
-            release("u%d_%d" % (m, j))
-            col = gam_t[:, NJ * m + j : NJ * m + j + 1]
-            if on_vector and not parts[j]:
-                piece = sb("part%d_%d" % (m, j), [P, TOK], F32)
-                nc.vector.tensor_scalar(out=piece[:], in0=bank[:], scalar1=col, scalar2=None, op0=MULT)
-                parts[j].append(piece)
-            elif on_vector:
-                acc = parts[j][0]
-                nc.vector.scalar_tensor_tensor(out=acc[:], in0=bank[:], scalar=col, in1=acc[:], op0=MULT, op1=ADD)
-            else:
-                piece = sb("part%d_%d" % (m, j), [P, TOK], F32)
-                nc.scalar.activation(out=piece[:], in_=bank[:], func=COPY, scale=col)
-                parts[j].append(piece)
+        def product_on_vector(m, j):
+            bank, gain = multiply_u(m, j, vector_ring)
+            total = parts[j][0]
+            nc.vector.scalar_tensor_tensor(out=total[:], in0=bank[:], scalar=gain, in1=total[:], op0=MULT, op1=ADD)
 
-        def pool_add(j, fresh=None):
+        def product_on_scalar(m, j):
+            bank, gain = multiply_u(m, j, free_banks)
+            part = sb("part%d_%d" % (m, j), [P, TOK], F32)
+            nc.scalar.activation(out=part[:], in_=bank[:], func=COPY, scale=gain)
+            parts[j].append(part)
+
+        def add_on_gpsimd(j, buffer_of=None):
             last = parts[j].pop()
-            acc = parts[j][0 if j < SEEDED else 1]
-            total = acc
-            if fresh:
-                total = keep.tile([P, TOK], F32, name="sum%d" % j, tag=fresh, align_bytes=64)
-                parts[j][0] = total
-            nc.gpsimd.tensor_tensor(out=total[:], in0=acc[:], in1=last[:], op=ADD)
+            other = parts[j].pop()
+            total = sb("sum_in_" + buffer_of, [P, TOK], F32, buffer_of) if buffer_of else other
+            nc.gpsimd.tensor_tensor(out=total[:], in0=other[:], in1=last[:], op=ADD)
+            parts[j].append(total)
 
-        def turn_parts(j, last, keep_first=False, plain=0):
-            first = j not in out_bank
-            if first:
-                out_bank[j] = new_bank("o%d" % j, [P, TT, P])
-            order = list(reversed(parts[j][1:] if keep_first else parts[j]))
-            kept = parts[j][:1] if keep_first else []
-            parts[j].clear()
-            parts[j].extend(kept)
-            for n, piece in enumerate(order):
+        def turn_result(j):
+            bank = take_bank("out%d" % j, [P, TT, P])
+            order = list(reversed(parts[j]))
+            for n, part in enumerate(order):
                 for i in range(TT):
                     nc.tensor.matmul(
-                        out_bank[j][:, i, :],
-                        lhsT=piece[:, P * i : P * (i + 1)],
+                        bank[:, i, :],
+                        lhsT=part[:, P * i : P * (i + 1)],
                         rhs=ident[:],
-                        start=(first and n == 0 and i == 0),
-                        stop=(last and n == len(order) - 1 and i == TT - 1),
-                        is_transpose=(n > 0 or i >= plain),
+                        start=(n == 0 and i == 0),
+                        stop=(n == len(order) - 1 and i == TT - 1),
+                        is_transpose=True,
                     )
+            return give_back("out%d" % j)
 
-        def drain_out(j, on_vector=False):
-            bank = out_bank[j]
-            release("o%d" % j)
-            copy = nc.vector.tensor_copy if on_vector else nc.scalar.copy
-            copy(out=o32[j // 2][:, :, P * (j % 2) : P * (j % 2 + 1)], in_=bank[:])
+        def out32_of(first, last):
+            return out32[first // 2][:, :, P * (first % 2) : P * (first % 2 + last - first)]
 
-        def store(j0, j1):
+        def store_result(first, last):
             nc.sync.dma_start(
-                out=out_0[:, P * j0 : P * j1].rearrange("(i p) f -> p i f", p=P),
-                in_=o32[j0 // 2][:, :, P * (j0 % 2) : P * (j0 % 2 + j1 - j0)],
+                out=out_0[:, P * first : P * last].rearrange("(i p) f -> p i f", p=P), in_=out32_of(first, last)
             )
 
-        def round_bank(bank, j, i0, i1, copy):
-            q0 = 32 * (j % 4)
-            dst = o16[j // 4][:].rearrange("p u i (q e) -> p u i q e", e=2)[:, :, i0:i1, q0 : q0 + 32, :]
-            copy(out=dst, in_=bank[:].rearrange("p i (q u e) -> p u i q e", u=2, e=2))
+        def rounding_views(source, first, last):
+            q = 32 * (first % 4)
+            dst = out16[first // 4][:].rearrange("p u i (q e) -> p u i q e", e=2)[:, :, :, q : q + 32 * (last - first), :]
+            return dst, source.rearrange("p i (q u e) -> p u i q e", u=2, e=2)
 
-        def last_tiles():
-            turn_parts(6, True)
-            round_bank(out_bank[6], 6, 0, TT, nc.vector.tensor_copy if LAST_V else nc.scalar.copy)
-            drain_out(6)
-            halves = []
-            for h in range(2):
-                bank = new_bank("o7_%d" % h, [P, 2, P])
-                halves.append(bank)
-                for ii in range(2):
-                    i = 2 * h + ii
-                    nc.tensor.transpose(bank[:, ii, :], parts[7][0][:, P * i : P * (i + 1)], ident[:])
-                round_bank(bank, 7, 2 * h, 2 * h + 2, nc.vector.tensor_copy)
-            for h in range(2):
-                nc.scalar.copy(out=o32[3][:, 2 * h : 2 * h + 2, P : 2 * P], in_=halves[h][:])
-                release("o7_%d" % h)
-
-        def store_last():
-            for h in range(2):
-                nc.sync.dma_start(
-                    out=out_0[256 * h : 256 * (h + 1), 6 * P : 8 * P].rearrange("(i p) f -> p i f", p=P),
-                    in_=o32[3][:, 2 * h : 2 * h + 2, :],
-                )
-
-        def round_out(j0, j1, on_vector=True):
-            q0 = 32 * (j0 % 4)
-            dst = o16[j0 // 4][:].rearrange("p u i (q e) -> p u i q e", e=2)[:, :, :, q0 : q0 + 32 * (j1 - j0), :]
-            src = o32[j0 // 2][:, :, P * (j0 % 2) : P * (j0 % 2 + j1 - j0)].rearrange("p i (q u e) -> p u i q e", u=2, e=2)
-            if on_vector == 2:
-                nc.gpsimd.tensor_scalar(out=dst, in0=src, scalar1=1.0, scalar2=-0.0, op0=MULT, op1=ADD)
-            else:
-                copy = nc.vector.tensor_copy if on_vector else nc.scalar.copy
-                copy(out=dst, in_=src)
-
-        def mm_plane(g, h):
-            bank = new_bank("pt%d_%d" % (g, h), [P, 2, 2, P])
-            held[("plane", g, h)] = bank
+        def turn_plane(g, h, copy):
+            bank = take_bank("plane%d_%d" % (g, h), [P, 2, 2, P])
             for ii in range(2):
                 for u in range(2):
-                    nc.tensor.transpose(bank[:, ii, u, :], o16[g][:, u, 2 * h + ii, :].bitcast(F32), ident[:])
+                    nc.tensor.transpose(bank[:, ii, u, :], out16[g][:, u, 2 * h + ii, :].bitcast(F32), ident[:])
+            give_back("plane%d_%d" % (g, h))
+            dst = p_words[(g, h)][:].rearrange("p n t -> p (n t)").bitcast(F32)
+            copy(out=dst.rearrange("p (i n u) -> p i n u", i=2, u=2), in_=bank[:].rearrange("p i u n -> p i n u"))
 
-        def drain_plane(g, h, on_vector=False):
-            bank = held.pop(("plane", g, h))
-            release("pt%d_%d" % (g, h))
-            dst = pg[(g, h)][:].rearrange("p n t -> p (n t)").bitcast(F32)
-            dst = dst.rearrange("p (i n u) -> p i n u", i=2, u=2)
-            copy = nc.vector.tensor_copy if on_vector else nc.scalar.copy
-            copy(out=dst, in_=bank[:].rearrange("p i u n -> p i n u"))
-
-        def plane_quant(g, h):
-            sl = slice(256 * h, 256 * (h + 1))
+        def quantise_plane(g, h):
+            tokens = slice(2 * P * h, 2 * P * (h + 1))
             nc.vector.quantize_mx(
-                out=pq[g][:, sl].bitcast(FP8X4), scales=ps[4 * g : P, sl], in_=pg[(g, h)][:].rearrange("p n t -> p (n t)")
+                out=p_codes[g][:, tokens].bitcast(FP8X4),
+                scales=p_plane[4 * g : P, tokens],
+                in_=p_words[(g, h)][:].rearrange("p n t -> p (n t)"),
             )
 
-        def plane_store(g, h0=0, h1=2):
-            sl = slice(256 * h0, 256 * h1)
-            nc.sync.dma_start(
-                out=out_1[g].rearrange("p n t -> p (n t)").bitcast(I32)[:, sl], in_=pq[g][:, sl].bitcast(I32)
-            )
-
-        def scale_store():
-            for q in range(4):
-                nc.scalar.dma_start(
-                    out=out_2[:, 4 * q : 4 * q + 4, :].bitcast(I32), in_=ps[32 * q : 32 * q + 8, :].bitcast(I32)
-                )
-
-        def stage1(m, i):
-            mm_h(m, i)
-            drain_h(m, i)
-
-        def stage2(m, j, on_vector):
-            mm_u(m, j, vector_ring if on_vector else free_banks)
-            drain_u(m, j, on_vector)
-
-        def base(j):
-            mm_base(j)
-            drain_base(j)
-
-        def x_turn(i):
-            mm_x(i)
-            drain_x(i)
-
-        def out_turn(j, on_vector=False):
-            turn_parts(j, True, False, PLAIN[j])
-            drain_out(j, on_vector)
-
-        def plane_turn(g, h, on_vector=False):
-            mm_plane(g, h)
-            drain_plane(g, h, on_vector)
-
-        def out_last(j):
-            turn_parts(j, True)
-            round_bank(out_bank[j], j, 0, TT, nc.vector.tensor_copy)
-            drain_out(j)
-
-        nc.vector.memset(lam_rows[:], 0.0)
-        nc.vector.memset(gam_rows[:], 0.0)
-        make_identity(nc, ident[:])
-        nc.gpsimd.memset(w0s[:].rearrange("p g n -> p (g n)").bitcast(I32), 0)
-        nc.gpsimd.memset(aws[:].bitcast(I32), 0)
-        nc.scalar.dma_start(out=lam_rows[0:NB, :].bitcast(BF16), in_=lam[:, :])
-        nc.scalar.dma_start(out=gam_rows[0 : NB * NJ, :], in_=gam.rearrange("m (j p) -> (m j) p", p=P))
-        nc.scalar.activation(out=ident_b[:], in_=ident[:], func=COPY)
-        load_b(0, 0)
-        load_x(0)
-        load_b(0, 1)
-        load_x(1)
-        load_x(2)
-        load_x(3)
-        load_b(1, 0)
-        load_b(1, 1)
-        load_b(2, 0)
-        load_b(2, 1)
-        load_w0_scales()
-        nc.sync.dma_start(out=w0[:].bitcast(I32), in_=w0_words.rearrange("g p b -> p g b").bitcast(I32))
-        load_b(3, 0)
-        load_b(3, 1)
-        load_a_scales()
-        nc.sync.dma_start(out=aw[:].bitcast(I32), in_=a_words[0].bitcast(I32))
-
-        inter_s(0, 0)
-        inter_v(0, 0)
-        quant_b(0, 0)
-        x_turn(0)
-        inter_v(0, 1)
-        inter_s(0, 1)
-        quant_b(0, 1)
-        x_turn(1)
-        lam_turn()
-        gam_turn()
-        quant_x(0)
-        x_turn(2)
-        x_turn(3)
-        inter_v(1, 0)
-        inter_s(1, 0)
-        inter_s(1, 1)
-        quant_x(1)
-
-        def side_work(steps):
-            for kind, j in steps:
-                if kind == "mm":
-                    mm_base(j)
-                elif kind == "drain":
-                    drain_base(j)
-                elif kind == "base":
-                    base(j)
-                else:
-                    stage2(kind, j, False)
-                    if (kind, j) in EARLY_ADDS:
-                        pool_add(j, "bgr_late" if (kind, j) == EARLY_ADDS[0] else None)
+        interleave_scalar(0, 0)
+        interleave_helper(0, 0)
+        quantise_basis(0, 0)
+        turn_x(0)
+        interleave_helper(0, 1)
+        interleave_scalar(0, 1)
+        quantise_basis(0, 1)
+        turn_x(1)
+        turn_lam_and_gam()
+        quantise_x(0)
+        turn_x(2)
+        turn_x(3)
+        interleave_helper(1, 0)
+        interleave_scalar(1, 0)
+        interleave_scalar(1, 1)
+        quantise_x(1)
 
         for m in range(NB):
-            more = m + 1 < NB
-            mm_h(m, 0)
-            mm_h(m, 1)
-            side_work(MID[m])
-            mm_h(m, 2)
-            mm_h(m, 3)
+            multiply_h(m, 0)
+            multiply_h(m, 1)
+            if m == 1:
+                for j in (0, 1):
+                    multiply_base(j)
+                    drain_base(j)
+            if m == 2:
+                drain_base(2)
+                drain_base(3)
+            if m == 3:
+                drain_base(4)
+                product_on_scalar(0, 4)
+                add_on_gpsimd(4)
+                drain_base(5)
+            multiply_h(m, 2)
+            multiply_h(m, 3)
             drain_h(m, 0)
             drain_h(m, 1)
             if m == 0:
-                inter_v(1, 1)
-            elif more:
-                inter_rest(m + 1, 1)
-                quant_h(m - 1)
-            if more:
-                quant_b(m + 1, 0)
-                quant_b(m + 1, 1)
-            side_work(SIDE[m])
+                interleave_helper(1, 1)
+            if m in (1, 2):
+                quantise_hl(m - 1)
+            if m + 1 < NB:
+                quantise_basis(m + 1, 0)
+                quantise_basis(m + 1, 1)
+            if m == 2:
+                product_on_scalar(0, 2)
+                add_on_gpsimd(2, "b_words_second")
+                product_on_scalar(0, 3)
+                add_on_gpsimd(3)
+            if m in (1, 2):
+                multiply_base(2 * m)
+                multiply_base(2 * m + 1)
             if m + 2 < NB:
-                inter_v(m + 2, 1)
-                inter_s(m + 2, 0)
+                interleave_helper(m + 2, 1)
+                interleave_scalar(m + 2, 0)
+                interleave_scalar(m + 2, 1)
             drain_h(m, 2)
             drain_h(m, 3)
 
-        stream = [(term, j + k) for j in range(0, NJ, 2) for term in range(NB) for k in range(2)]
-        stream = [unit for unit in stream if unit not in ON_SCALAR]
-        for k in range(RING):
+        for_vector = [
+            (m, j + k) for j in range(0, NJ, 2) for m in range(NB) for k in range(2) if j < FIRST_SHARED or m >= 2
+        ]
+        for_scalar = [(1, 2), (1, 3), (0, 5), (1, 4), (1, 5), (None, 6), (None, 7), (0, 6), (1, 6), (0, 7), (1, 7)]
+        for k in range(VECTOR_BANKS):
             vector_ring.append(free_banks.pop(0))
-        side = list(LATE)
-        adds = list(LATE_ADDS)
-        for pos, (term, j) in enumerate(stream):
-            stage2(term, j, True)
+        for pos, (m, j) in enumerate(for_vector):
+            product_on_vector(m, j)
             if pos == 0:
-                quant_h(2)
-                quant_h(3)
-            if side:
-                side_work([side.pop(0)])
-            while adds and adds[0] not in side:
-                pool_add(adds[0][1], "hl3" if len(adds) == len(LATE_ADDS) else None)
-                adds.pop(0)
-            for k in TURN_AT.get(pos, ()):
-                out_turn(k)
-                if k % 2 == 1:
-                    store(k - 1, k + 1)
-                    round_out(k - 1, k + 1, ROUND_ON[k // 2])
-            for g, h in PLANE_AT.get(pos - len(stream), ()):
-                plane_turn(g, h)
+                quantise_hl(2)
+                quantise_hl(3)
+            if pos < len(for_scalar):
+                late_m, late_j = for_scalar[pos]
+                if late_m is None:
+                    multiply_base(late_j)
+                    drain_base(late_j)
+                else:
+                    product_on_scalar(late_m, late_j)
+                    if late_j < FIRST_TWO_PARTS or late_m == 1:
+                        add_on_gpsimd(late_j, "hl3" if pos == 0 else None)
+            done_m, done_j = for_vector[max(pos - AHEAD, 0)]
+            if done_m == NB - 1 and done_j % 2 == 1:
+                first = done_j - 1
+                for k in (first, first + 1):
+                    nc.scalar.copy(out=out32_of(k, k + 1), in_=turn_result(k)[:])
+                store_result(first, first + 2)
+                dst, src = rounding_views(out32_of(first, first + 2), first, first + 2)
+                if first < 4:
+                    nc.gpsimd.tensor_scalar(out=dst, in0=src, scalar1=1.0, scalar2=-0.0, op0=MULT, op1=ADD)
+                else:
+                    nc.scalar.copy(out=dst, in_=src)
+
         free_banks.extend(vector_ring)
-        plane_quant(0, 0)
-        plane_store(0, 0, 1)
-        out_last(6)
-        store(6, 7)
-        out_last(7)
-        plane_quant(0, 1)
-        plane_store(0, 1, 2)
-        store(7, 8)
-        plane_turn(1, 0, True)
-        plane_turn(1, 1)
-        plane_quant(1, 0)
-        plane_quant(1, 1)
-        plane_store(1)
-        scale_store()
+        for j in (NJ - 2, NJ - 1):
+            bank = turn_result(j)
+            dst, src = rounding_views(bank[:], j, j + 1)
+            nc.vector.tensor_copy(out=dst, in_=src)
+            nc.scalar.copy(out=out32_of(j, j + 1), in_=bank[:])
+            store_result(j, j + 1)
+        for g in range(2):
+            turn_plane(g, 0, nc.vector.tensor_copy)
+            turn_plane(g, 1, nc.scalar.copy)
+        for g in range(2):
+            quantise_plane(g, 0)
+            quantise_plane(g, 1)
+            nc.sync.dma_start(out=out_1[g].rearrange("p n t -> p (n t)").bitcast(I32), in_=p_codes[g][:].bitcast(I32))
+        for q in range(4):
+            nc.scalar.dma_start(
+                out=out_2[:, 4 * q : 4 * q + 4, :].bitcast(I32), in_=p_plane[32 * q : 32 * q + 8, :].bitcast(I32)
+            )

@@ -23,7 +23,7 @@ TT = TOK // P
 NJ = F // P
 PIECES = R // 8
 
-HELPER_PIECES = {(0, 0): 40, (0, 1): 40, (1, 0): 24, (1, 1): 24, (2, 0): 0, (2, 1): 44, (3, 0): 0, (3, 1): 44}
+HELPER_PIECES = {(0, 0): 40, (0, 1): 40, (1, 0): 24, (1, 1): 24, (2, 0): 0, (2, 1): 48, (3, 0): 0, (3, 1): 48}
 FIRST_SHARED = 2
 FIRST_TWO_PARTS = 6
 VECTOR_BANKS = 4
@@ -135,7 +135,7 @@ def tile_randlorafullrankbasissum_x2_kernel(
 
         def interleave_helper(m, g):
             if m < 2:
-                dst, src = interleave_views(m, g, "c t i j", 0, HELPER_PIECES[(m, g)])
+                dst, src = interleave_views(m, g, "(c i) j t", 0, HELPER_PIECES[(m, g)])
                 nc.vector.tensor_copy(out=dst, in_=src)
             else:
                 dst, src = interleave_views(m, g, "(c i) t j", 0, HELPER_PIECES[(m, g)])
@@ -261,19 +261,21 @@ def tile_randlorafullrankbasissum_x2_kernel(
             nc.gpsimd.tensor_tensor(out=total[:], in0=other[:], in1=last[:], op=ADD)
             parts[j].append(total)
 
-        def turn_result(j):
-            bank = take_bank("out%d" % j, [P, TT, P])
-            order = list(reversed(parts[j]))
-            for n, part in enumerate(order):
+        def turn_parts(j, some, opens, closes):
+            bank = take_bank("out%d" % j, [P, TT, P]) if opens else in_use["out%d" % j][0]
+            for n, part in enumerate(some):
                 for i in range(TT):
                     nc.tensor.matmul(
                         bank[:, i, :],
                         lhsT=part[:, P * i : P * (i + 1)],
                         rhs=ident[:],
-                        start=(n == 0 and i == 0),
-                        stop=(n == len(order) - 1 and i == TT - 1),
+                        start=(opens and n == 0 and i == 0),
+                        stop=(closes and n == len(some) - 1 and i == TT - 1),
                         is_transpose=True,
                     )
+
+        def turn_result(j):
+            turn_parts(j, parts[j][:1], j < FIRST_TWO_PARTS, True)
             return give_back("out%d" % j)
 
         def out32_of(first, last):
@@ -306,6 +308,12 @@ def tile_randlorafullrankbasissum_x2_kernel(
                 in_=p_words[(g, h)][:].rearrange("p n t -> p (n t)"),
             )
 
+        def store_codes(g, first, last):
+            tokens = slice(2 * P * first, 2 * P * last)
+            nc.sync.dma_start(
+                out=out_1[g].rearrange("p n t -> p (n t)").bitcast(I32)[:, tokens], in_=p_codes[g][:, tokens].bitcast(I32)
+            )
+
         interleave_scalar(0, 0)
         interleave_helper(0, 0)
         quantise_basis(0, 0)
@@ -333,11 +341,6 @@ def tile_randlorafullrankbasissum_x2_kernel(
             if m == 2:
                 drain_base(2)
                 drain_base(3)
-            if m == 3:
-                drain_base(4)
-                product_on_scalar(0, 4)
-                add_on_gpsimd(4)
-                drain_base(5)
             multiply_h(m, 2)
             multiply_h(m, 3)
             drain_h(m, 0)
@@ -354,9 +357,16 @@ def tile_randlorafullrankbasissum_x2_kernel(
                 add_on_gpsimd(2, "b_words_second")
                 product_on_scalar(0, 3)
                 add_on_gpsimd(3)
-            if m in (1, 2):
-                multiply_base(2 * m)
-                multiply_base(2 * m + 1)
+                multiply_base(4)
+                drain_base(4)
+                product_on_scalar(0, 4)
+                add_on_gpsimd(4)
+            if m == 3:
+                multiply_base(5)
+                drain_base(5)
+            if m == 1:
+                multiply_base(2)
+                multiply_base(3)
             if m + 2 < NB:
                 interleave_helper(m + 2, 1)
                 interleave_scalar(m + 2, 0)
@@ -398,6 +408,8 @@ def tile_randlorafullrankbasissum_x2_kernel(
 
         free_banks.extend(vector_ring)
         for j in (NJ - 2, NJ - 1):
+            turn_parts(j, parts[j][1:], True, False)
+        for j in (NJ - 2, NJ - 1):
             bank = turn_result(j)
             dst, src = rounding_views(bank[:], j, j + 1)
             nc.vector.tensor_copy(out=dst, in_=src)
@@ -406,10 +418,12 @@ def tile_randlorafullrankbasissum_x2_kernel(
         for g in range(2):
             turn_plane(g, 0, nc.vector.tensor_copy)
             turn_plane(g, 1, nc.scalar.copy)
-        for g in range(2):
-            quantise_plane(g, 0)
-            quantise_plane(g, 1)
-            nc.sync.dma_start(out=out_1[g].rearrange("p n t -> p (n t)").bitcast(I32), in_=p_codes[g][:].bitcast(I32))
+        quantise_plane(0, 0)
+        quantise_plane(0, 1)
+        store_codes(0, 0, 2)
+        for h in range(2):
+            quantise_plane(1, h)
+            store_codes(1, h, h + 1)
         for q in range(4):
             nc.scalar.dma_start(
                 out=out_2[:, 4 * q : 4 * q + 4, :].bitcast(I32), in_=p_plane[32 * q : 32 * q + 8, :].bitcast(I32)

@@ -40,7 +40,7 @@ def tile_randlorafullrankbasissum_x2_kernel(
         ctx.enter_context(tc.manual_schedule())
 
         def sb(name, shape, dtype, tag=None):
-            return keep.tile(shape, dtype, name=name, tag=tag or name, align_bytes=64)
+            return keep.tile(shape, dtype, name=name, tag=tag or name, align_bytes=256)
 
         free_banks = list(range(8))
         vector_ring = []

@@ -128,21 +128,21 @@ def tile_randlorafullrankbasissum_x2_kernel(
             if (m, g) not in b_words:
                 tag = "b_words_second" if g == 1 and m > 0 else None
                 b_words[(m, g)] = sb("b_words%d_%d" % (m, g), [P, 4 * R], BF16, tag)
-            dst = b_words[(m, g)][:].rearrange("p (t c i j) -> p " + walk, t=4, i=2, j=4)
-            src = b_rows[(m, g)][:].rearrange("p j (c i t) -> p " + walk, i=2, t=4)
+            dst = b_words[(m, g)][:].rearrange("p (t c i h e) -> p " + walk, t=4, i=2, h=2, e=2)
+            src = b_rows[(m, g)][:].rearrange("p (h e) (c i t) -> p " + walk, i=2, t=4, e=2)
             step = dst.shape[1] // PIECES
             return dst[:, step * first : step * last], src[:, step * first : step * last]
 
         def interleave_helper(m, g):
             if m < 2:
-                dst, src = interleave_views(m, g, "(c i) j t", 0, HELPER_PIECES[(m, g)])
+                dst, src = interleave_views(m, g, "(c i) h t e", 0, HELPER_PIECES[(m, g)])
                 nc.vector.tensor_copy(out=dst, in_=src)
             else:
-                dst, src = interleave_views(m, g, "(c i) t j", 0, HELPER_PIECES[(m, g)])
+                dst, src = interleave_views(m, g, "(c i) t (h e)", 0, HELPER_PIECES[(m, g)])
                 nc.gpsimd.tensor_scalar(out=dst, in0=src, scalar1=1.0, scalar2=-0.0, op0=MULT, op1=ADD)
 
         def interleave_scalar(m, g):
-            dst, src = interleave_views(m, g, "(c i) j t", HELPER_PIECES[(m, g)], PIECES)
+            dst, src = interleave_views(m, g, "(c i) h t e", HELPER_PIECES[(m, g)], PIECES)
             nc.scalar.copy(out=dst, in_=src)
 
         def quantise_basis(m, g):

@@ -334,15 +334,16 @@ def tile_randlorafullrankbasissum_x2_kernel(
         for m in range(NB):
             multiply_h(m, 0)
             multiply_h(m, 1)
+            multiply_h(m, 2)
+            multiply_h(m, 3)
             if m == 1:
-                for j in (0, 1):
-                    multiply_base(j)
-                    drain_base(j)
+                multiply_base(0)
+                multiply_base(1)
+            if m == 2:
+                multiply_base(3)
             if m == 2:
                 drain_base(2)
                 drain_base(3)
-            multiply_h(m, 2)
-            multiply_h(m, 3)
             drain_h(m, 0)
             drain_h(m, 1)
             if m == 0:
@@ -366,10 +367,12 @@ def tile_randlorafullrankbasissum_x2_kernel(
                 drain_base(5)
             if m == 1:
                 multiply_base(2)
-                multiply_base(3)
             if m + 2 < NB:
                 interleave_helper(m + 2, 1)
                 interleave_scalar(m + 2, 0)
+                if m == 1:
+                    drain_base(0)
+                    drain_base(1)
                 interleave_scalar(m + 2, 1)
             drain_h(m, 2)
             drain_h(m, 3)

@@ -75,9 +75,10 @@ def tile_randlorafullrankbasissum_x2_kernel(
         gam_t = sb("gam_t", [P, NB * NJ], F32)
         ident = sb("ident", [P, P], F32)
         ident_b = sb("ident_b", [P, P], BF16)
-        hl = [sb("hl%d" % m, [P, TOK, 4], BF16) for m in range(NB)]
-        hl_codes = [sb("hl_codes%d" % m, [P, TOK], U32) for m in range(NB)]
-        hl_scales = [sb("hl_scales%d" % m, [P, TOK], U8) for m in range(NB)]
+        hl_late = (sb("hl3", [P, 2, TOK, 4], BF16), sb("hl_codes23", [P, 2, TOK], U32), sb("hl_scales23", [P, 2, TOK], U8))
+        hl = [sb("hl%d" % m, [P, TOK, 4], BF16) for m in range(2)] + [hl_late[0][:, k, :, :] for k in range(2)]
+        hl_codes = [sb("hl_codes%d" % m, [P, TOK], U32) for m in range(2)] + [hl_late[1][:, k, :] for k in range(2)]
+        hl_scales = [sb("hl_scales%d" % m, [P, TOK], U8) for m in range(2)] + [hl_late[2][:, k, :] for k in range(2)]
         parts = [[] for j in range(NJ)]
         out32 = [sb("out32_%d" % pair, [P, TT, 2 * P], F32) for pair in range(NJ // 2)]
         out16 = [sb("out16_%d" % g, [P, 2, TT, 2 * P], BF16) for g in range(2)]
@@ -183,21 +184,22 @@ def tile_randlorafullrankbasissum_x2_kernel(
             nc.tensor.transpose(bank[:], gam_rows[:], ident_b[:])
             nc.vector.tensor_copy(out=gam_t[:], in_=give_back("gam")[:, 0 : NB * NJ])
 
-        def multiply_h(m, i):
-            bank = take_bank("h%d_%d" % (m, i), [P, 4, P])
-            tokens = slice(P * i, P * (i + 1))
-            for t in range(4):
-                cols = slice(P * t, P * (t + 1))
-                for g in range(KG):
-                    nc.tensor.matmul_mx(
-                        out=bank[:, t, :],
-                        lhsT=b_codes[m][:, g, cols].bitcast(FP8X4),
-                        lhsT_scale=b_scales[m][:, g, cols],
-                        rhs=x_codes[:, g, tokens].bitcast(FP8X4),
-                        rhs_scale=x_scales[:, g, tokens],
-                        start=(g == 0),
-                        stop=(g == KG - 1),
-                    )
+        def multiply_h(m, tiles):
+            banks = [take_bank("h%d_%d" % (m, i), [P, 4, P]) for i in tiles]
+            for g in range(KG):
+                for i, bank in zip(tiles, banks):
+                    tokens = slice(P * i, P * (i + 1))
+                    for t in range(4):
+                        cols = slice(P * t, P * (t + 1))
+                        nc.tensor.matmul_mx(
+                            out=bank[:, t, :],
+                            lhsT=b_codes[m][:, g, cols].bitcast(FP8X4),
+                            lhsT_scale=b_scales[m][:, g, cols],
+                            rhs=x_codes[:, g, tokens].bitcast(FP8X4),
+                            rhs_scale=x_scales[:, g, tokens],
+                            start=(g == 0 and t == 0),
+                            stop=(g == KG - 1 and t == 3),
+                        )
 
         def drain_h(m, i):
             nc.vector.tensor_tensor(
@@ -322,9 +324,9 @@ def tile_randlorafullrankbasissum_x2_kernel(
         interleave_scalar(0, 1)
         quantise_basis(0, 1)
         turn_x(1)
-        turn_lam_and_gam()
         quantise_x(0)
         turn_x(2)
+        turn_lam_and_gam()
         turn_x(3)
         interleave_helper(1, 0)
         interleave_scalar(1, 0)
@@ -332,10 +334,9 @@ def tile_randlorafullrankbasissum_x2_kernel(
         quantise_x(1)
 
         for m in range(NB):
-            multiply_h(m, 0)
-            multiply_h(m, 1)
-            multiply_h(m, 2)
-            multiply_h(m, 3)
+            multiply_h(m, [0, 1])
+            multiply_h(m, [2])
+            multiply_h(m, [3])
             if m == 1:
                 multiply_base(0)
                 multiply_base(1)
@@ -348,10 +349,11 @@ def tile_randlorafullrankbasissum_x2_kernel(
             drain_h(m, 1)
             if m == 0:
                 interleave_helper(1, 1)
+            if m + 1 < NB:
+                quantise_basis(m + 1, 0)
             if m in (1, 2):
                 quantise_hl(m - 1)
             if m + 1 < NB:
-                quantise_basis(m + 1, 0)
                 quantise_basis(m + 1, 1)
             if m == 2:
                 product_on_scalar(0, 2)
@@ -386,8 +388,11 @@ def tile_randlorafullrankbasissum_x2_kernel(
         for pos, (m, j) in enumerate(for_vector):
             product_on_vector(m, j)
             if pos == 0:
-                quantise_hl(2)
-                quantise_hl(3)
+                nc.vector.quantize_mx(
+                    out=hl_late[1][:].rearrange("p k n -> p (k n)").bitcast(FP8X4),
+                    scales=hl_late[2][:].rearrange("p k n -> p (k n)"),
+                    in_=hl_late[0][:].rearrange("p k n t -> p (k n t)"),
+                )
             if pos < len(for_scalar):
                 late_m, late_j = for_scalar[pos]
                 if late_m is None:

from contextlib import ExitStack

import concourse.mybir as mybir
from concourse.masks import make_identity

TOK, D, NB, R, F = 512, 1024, 4, 512, 1024
FLOPS = 2 * TOK * D * R * NB + 2 * TOK * R * F * NB + 2 * TOK * D * F

F32 = mybir.dt.float32
BF16 = mybir.dt.bfloat16
U32 = mybir.dt.uint32
I32 = mybir.dt.int32
U8 = mybir.dt.uint8
FP8X4 = mybir.dt.float8_e4m3fn_x4
FP4X4 = mybir.dt.float4_e2m1fn_x4
MULT = mybir.AluOpType.mult
ADD = mybir.AluOpType.add
COPY = mybir.ActivationFunctionType.Copy

P = 128
KG = D // 512
TT = TOK // P
NJ = F // P
PIECES = R // 8

HELPER_PIECES = {(0, 0): 40, (0, 1): 40, (1, 0): 24, (1, 1): 24, (2, 0): 0, (2, 1): 48, (3, 0): 0, (3, 1): 48}
FIRST_SHARED = 2
FIRST_TWO_PARTS = 6
VECTOR_BANKS = 4
AHEAD = 3


def tile_randlorafullrankbasissum_x2_kernel(
    tc, x, w0_words, w0_scales, bases, lam, a_words, a_scales, gam, out_0, out_1, out_2
):
    nc = tc.nc
    with ExitStack() as ctx:
        keep = ctx.enter_context(tc.tile_pool(name="keep", bufs=1))
        psum = ctx.enter_context(tc.psum_pool(name="psum", bufs=1))
        ctx.enter_context(tc.manual_schedule())

        def sb(name, shape, dtype, tag=None):
            return keep.tile(shape, dtype, name=name, tag=tag or name, align_bytes=256)

        free_banks = list(range(8))
        vector_ring = []
        in_use = {}

        def take_bank(name, shape, dtype=F32, ring=free_banks):
            number = ring.pop(0)
            bank = psum.tile(shape, dtype, name=name, tag="bank%d" % number)
            in_use[name] = (bank, number, ring)
            return bank

        def give_back(name):
            bank, number, ring = in_use.pop(name)
            ring.append(number)
            return bank

        x_rows = [sb("x_rows%d" % i, [P, D], BF16) for i in range(TT)]
        x_words = [sb("x_words%d" % h, [P, KG, 2 * P, 4], BF16) for h in range(2)]
        x_codes = sb("x_codes", [P, KG, TOK], U32)
        x_scales = sb("x_scales", [P, KG, TOK], U8)
        b_rows = {(m, g): sb("b_rows%d_%d" % (m, g), [P, 4, R], BF16) for m in range(NB) for g in range(KG)}
        b_words = {}
        b_codes = [sb("b_codes%d" % m, [P, KG, R], U32) for m in range(NB)]
        b_scales = [sb("b_scales%d" % m, [P, KG, R], U8) for m in range(NB)]
        w0_codes = sb("w0_codes", [P, KG, 2 * F], U8)
        w0_plane = sb("w0_plane", [P, KG, F], U8)
        a_codes = sb("a_codes", [P, 2 * F], U8)
        a_plane = sb("a_plane", [P, F], U8)
        lam_rows = sb("lam_rows", [P, R // 2], F32)
        gam_rows = sb("gam_rows", [P, P], BF16)
        lam_t = sb("lam_t", [P, NB, 1, 4], BF16)
        gam_t = sb("gam_t", [P, NB * NJ], F32)
        ident = sb("ident", [P, P], F32)
        ident_b = sb("ident_b", [P, P], BF16)
        hl_late = (sb("hl3", [P, 2, TOK, 4], BF16), sb("hl_codes23", [P, 2, TOK], U32), sb("hl_scales23", [P, 2, TOK], U8))
        hl = [sb("hl%d" % m, [P, TOK, 4], BF16) for m in range(2)] + [hl_late[0][:, k, :, :] for k in range(2)]
        hl_codes = [sb("hl_codes%d" % m, [P, TOK], U32) for m in range(2)] + [hl_late[1][:, k, :] for k in range(2)]
        hl_scales = [sb("hl_scales%d" % m, [P, TOK], U8) for m in range(2)] + [hl_late[2][:, k, :] for k in range(2)]
        parts = [[] for j in range(NJ)]
        out32 = [sb("out32_%d" % pair, [P, TT, 2 * P], F32) for pair in range(NJ // 2)]
        out16 = [sb("out16_%d" % g, [P, 2, TT, 2 * P], BF16) for g in range(2)]
        p_words = {(g, h): sb("p_words%d_%d" % (g, h), [P, 2 * P, 4], BF16) for g in range(2) for h in range(2)}
        p_codes = [sb("p_codes%d" % g, [P, TOK], U32) for g in range(2)]
        p_plane = sb("p_plane", [P, TOK], U8)

        def load_x(i):
            nc.sync.dma_start(out=x_rows[i][:], in_=x[P * i : P * (i + 1), :])

        def load_basis(m, g):
            nc.sync.dma_start(
                out=b_rows[(m, g)][:], in_=bases[m, 512 * g : 512 * (g + 1), :].rearrange("(p j) r -> p j r", j=4)
            )

        nc.vector.memset(lam_rows[:], 0.0)
        nc.vector.memset(gam_rows[:], 0.0)
        make_identity(nc, ident[:])
        nc.gpsimd.memset(w0_plane[:].rearrange("p g n -> p (g n)").bitcast(I32), 0)
        nc.gpsimd.memset(a_plane[:].bitcast(I32), 0)
        nc.scalar.dma_start(out=lam_rows[0:NB, :].bitcast(BF16), in_=lam[:, :])
        nc.scalar.dma_start(out=gam_rows[0 : NB * NJ, :], in_=gam.rearrange("m (j p) -> (m j) p", p=P))
        nc.scalar.activation(out=ident_b[:], in_=ident[:], func=COPY)

        load_basis(0, 0)
        load_x(0)
        load_basis(0, 1)
        for i in range(1, TT):
            load_x(i)
        for m in (1, 2):
            for g in range(KG):
                load_basis(m, g)
        for q in range(4):
            nc.sync.dma_start(
                out=w0_plane[32 * q : 32 * q + 4, :, :].bitcast(I32),
                in_=w0_scales[:, 4 * q : 4 * q + 4, :].rearrange("g q n -> q g n").bitcast(I32),
            )
        nc.sync.dma_start(out=w0_codes[:].bitcast(I32), in_=w0_words.rearrange("g p b -> p g b").bitcast(I32))
        for g in range(KG):
            load_basis(3, g)
        for q in range(4):
            nc.sync.dma_start(
                out=a_plane[32 * q : 32 * q + 4, :].bitcast(I32), in_=a_scales[0, 4 * q : 4 * q + 4, :].bitcast(I32)
            )
        nc.sync.dma_start(out=a_codes[:].bitcast(I32), in_=a_words[0].bitcast(I32))

        def interleave_views(m, g, walk, first, last):
            if (m, g) not in b_words:
                tag = "b_words_second" if g == 1 and m > 0 else None
                b_words[(m, g)] = sb("b_words%d_%d" % (m, g), [P, 4 * R], BF16, tag)
            dst = b_words[(m, g)][:].rearrange("p (t c i h e) -> p " + walk, t=4, i=2, h=2, e=2)
            src = b_rows[(m, g)][:].rearrange("p (h e) (c i t) -> p " + walk, i=2, t=4, e=2)
            step = dst.shape[1] // PIECES
            return dst[:, step * first : step * last], src[:, step * first : step * last]

        def interleave_helper(m, g):
            if m < 2:
                dst, src = interleave_views(m, g, "(c i) h t e", 0, HELPER_PIECES[(m, g)])
                nc.vector.tensor_copy(out=dst, in_=src)
            else:
                dst, src = interleave_views(m, g, "(c i) t (h e)", 0, HELPER_PIECES[(m, g)])
                nc.gpsimd.tensor_scalar(out=dst, in0=src, scalar1=1.0, scalar2=-0.0, op0=MULT, op1=ADD)

        def interleave_scalar(m, g):
            dst, src = interleave_views(m, g, "(c i) h t e", HELPER_PIECES[(m, g)], PIECES)
            nc.scalar.copy(out=dst, in_=src)

        def quantise_basis(m, g):
            nc.vector.quantize_mx(
                out=b_codes[m][:, g, :].bitcast(FP8X4), scales=b_scales[m][:, g, :], in_=b_words[(m, g)][:]
            )

        def turn_x(i):
            words = x_rows[i][:].bitcast(F32)
            bank = take_bank("x%d" % i, [P, KG, 2, P])
            for g in range(KG):
                for u in range(2):
                    nc.tensor.transpose(bank[:, g, u, :], words[:, 256 * g + u : 256 * (g + 1) : 2], ident[:])
            give_back("x%d" % i)
            dst = x_words[i // 2][:, :, P * (i % 2) : P * (i % 2 + 1), :].rearrange("p g n t -> p g (n t)").bitcast(F32)
            nc.scalar.copy(
                out=dst.rearrange("p g (n u) -> p g n u", u=2), in_=bank[:].rearrange("p g u n -> p g n u")
            )

        def quantise_x(h):
            tokens = slice(2 * P * h, 2 * P * (h + 1))
            for g in range(KG):
                nc.vector.quantize_mx(
                    out=x_codes[:, g, tokens].bitcast(FP8X4),
                    scales=x_scales[:, g, tokens],
                    in_=x_words[h][:, g, :, :].rearrange("p n t -> p (n t)"),
                )

        def turn_lam_and_gam():
            bank = take_bank("lam", [P, 2, P])
            for u in range(2):
                nc.tensor.transpose(bank[:, u, :], lam_rows[:, u : R // 2 : 2], ident[:])
            nc.vector.tensor_copy(
                out=lam_t[:].rearrange("p m o t -> p m (o t)").bitcast(F32),
                in_=give_back("lam")[:, :, 0:NB].rearrange("p u m -> p m u"),
            )
            bank = take_bank("gam", [P, P], BF16)
            nc.tensor.transpose(bank[:], gam_rows[:], ident_b[:])
            nc.vector.tensor_copy(out=gam_t[:], in_=give_back("gam")[:, 0 : NB * NJ])

        def multiply_h(m, tiles):
            banks = [take_bank("h%d_%d" % (m, i), [P, 4, P]) for i in tiles]
            for g in range(KG):
                for i, bank in zip(tiles, banks):
                    tokens = slice(P * i, P * (i + 1))
                    for t in range(4):
                        cols = slice(P * t, P * (t + 1))
                        nc.tensor.matmul_mx(
                            out=bank[:, t, :],
                            lhsT=b_codes[m][:, g, cols].bitcast(FP8X4),
                            lhsT_scale=b_scales[m][:, g, cols],
                            rhs=x_codes[:, g, tokens].bitcast(FP8X4),
                            rhs_scale=x_scales[:, g, tokens],
                            start=(g == 0 and t == 0),
                            stop=(g == KG - 1 and t == 3),
                        )

        def drain_h(m, i):
            nc.vector.tensor_tensor(
                out=hl[m][:, P * i : P * (i + 1), :],
                in0=give_back("h%d_%d" % (m, i))[:].rearrange("p t n -> p n t"),
                in1=lam_t[:, m, :, :].to_broadcast([P, P, 4]),
                op=MULT,
            )

        def quantise_hl(m):
            nc.vector.quantize_mx(
                out=hl_codes[m][:].bitcast(FP8X4), scales=hl_scales[m][:], in_=hl[m][:].rearrange("p n t -> p (n t)")
            )

        def multiply_base(j):
            bank = take_bank("base%d" % j, [P, TOK])
            for g in range(KG):
                nc.tensor.matmul_mx(
                    out=bank[:],
                    lhsT=w0_codes[:, g, 2 * P * j : 2 * P * (j + 1)].bitcast(FP4X4),
                    lhsT_scale=w0_plane[:, g, P * j : P * (j + 1)],
                    rhs=x_codes[:, g, :].bitcast(FP8X4),
                    rhs_scale=x_scales[:, g, :],
                    start=(g == 0),
                    stop=(g == KG - 1),
                )

        def drain_base(j):
            part = sb("base_part%d" % j, [P, TOK], F32)
            nc.scalar.copy(out=part[:], in_=give_back("base%d" % j)[:])
            parts[j].append(part)

        def multiply_u(m, j, ring):
            bank = take_bank("u%d_%d" % (m, j), [P, TOK], F32, ring)
            nc.tensor.matmul_mx(
                out=bank[:],
                lhsT=a_codes[:, 2 * P * j : 2 * P * (j + 1)].bitcast(FP4X4),
                lhsT_scale=a_plane[:, P * j : P * (j + 1)],
                rhs=hl_codes[m][:].bitcast(FP8X4),
                rhs_scale=hl_scales[m][:],
                start=True,
                stop=True,
            )
            return give_back("u%d_%d" % (m, j)), gam_t[:, NJ * m + j : NJ * m + j + 1]

        def product_on_vector(m, j):
            bank, gain = multiply_u(m, j, vector_ring)
            total = parts[j][0]
            nc.vector.scalar_tensor_tensor(out=total[:], in0=bank[:], scalar=gain, in1=total[:], op0=MULT, op1=ADD)

        def product_on_scalar(m, j):
            bank, gain = multiply_u(m, j, free_banks)
            part = sb("part%d_%d" % (m, j), [P, TOK], F32)
            nc.scalar.activation(out=part[:], in_=bank[:], func=COPY, scale=gain)
            parts[j].append(part)

        def add_on_gpsimd(j, buffer_of=None):
            last = parts[j].pop()
            other = parts[j].pop()
            total = sb("sum_in_" + buffer_of, [P, TOK], F32, buffer_of) if buffer_of else other
            nc.gpsimd.tensor_tensor(out=total[:], in0=other[:], in1=last[:], op=ADD)
            parts[j].append(total)

        def turn_parts(j, some, opens, closes):
            bank = take_bank("out%d" % j, [P, TT, P]) if opens else in_use["out%d" % j][0]
            for n, part in enumerate(some):
                for i in range(TT):
                    nc.tensor.matmul(
                        bank[:, i, :],
                        lhsT=part[:, P * i : P * (i + 1)],
                        rhs=ident[:],
                        start=(opens and n == 0 and i == 0),
                        stop=(closes and n == len(some) - 1 and i == TT - 1),
                        is_transpose=True,
                    )

        def turn_result(j):
            turn_parts(j, parts[j][:1], j < FIRST_TWO_PARTS, True)
            return give_back("out%d" % j)

        def out32_of(first, last):
            return out32[first // 2][:, :, P * (first % 2) : P * (first % 2 + last - first)]

        def store_result(first, last):
            nc.sync.dma_start(
                out=out_0[:, P * first : P * last].rearrange("(i p) f -> p i f", p=P), in_=out32_of(first, last)
            )

        def rounding_views(source, first, last):
            q = 32 * (first % 4)
            dst = out16[first // 4][:].rearrange("p u i (q e) -> p u i q e", e=2)[:, :, :, q : q + 32 * (last - first), :]
            return dst, source.rearrange("p i (q u e) -> p u i q e", u=2, e=2)

        def turn_plane(g, h, copy):
            bank = take_bank("plane%d_%d" % (g, h), [P, 2, 2, P])
            for ii in range(2):
                for u in range(2):
                    nc.tensor.transpose(bank[:, ii, u, :], out16[g][:, u, 2 * h + ii, :].bitcast(F32), ident[:])
            give_back("plane%d_%d" % (g, h))
            dst = p_words[(g, h)][:].rearrange("p n t -> p (n t)").bitcast(F32)
            copy(out=dst.rearrange("p (i n u) -> p i n u", i=2, u=2), in_=bank[:].rearrange("p i u n -> p i n u"))

        def quantise_plane(g, h):
            tokens = slice(2 * P * h, 2 * P * (h + 1))
            nc.vector.quantize_mx(
                out=p_codes[g][:, tokens].bitcast(FP8X4),
                scales=p_plane[4 * g : P, tokens],
                in_=p_words[(g, h)][:].rearrange("p n t -> p (n t)"),
            )

        def store_codes(g, first, last):
            tokens = slice(2 * P * first, 2 * P * last)
            nc.sync.dma_start(
                out=out_1[g].rearrange("p n t -> p (n t)").bitcast(I32)[:, tokens], in_=p_codes[g][:, tokens].bitcast(I32)
            )

        interleave_scalar(0, 0)
        interleave_helper(0, 0)
        quantise_basis(0, 0)
        turn_x(0)
        interleave_helper(0, 1)
        interleave_scalar(0, 1)
        quantise_basis(0, 1)
        turn_x(1)
        quantise_x(0)
        turn_x(2)
        turn_lam_and_gam()
        turn_x(3)
        interleave_helper(1, 0)
        interleave_scalar(1, 0)
        interleave_scalar(1, 1)
        quantise_x(1)

        for m in range(NB):
            multiply_h(m, [0, 1])
            multiply_h(m, [2])
            multiply_h(m, [3])
            if m == 1:
                multiply_base(0)
                multiply_base(1)
            if m == 2:
                multiply_base(3)
            if m == 2:
                drain_base(2)
                drain_base(3)
            drain_h(m, 0)
            drain_h(m, 1)
            if m == 0:
                interleave_helper(1, 1)
            if m + 1 < NB:
                quantise_basis(m + 1, 0)
            if m in (1, 2):
                quantise_hl(m - 1)
            if m + 1 < NB:
                quantise_basis(m + 1, 1)
            if m == 2:
                product_on_scalar(0, 2)
                add_on_gpsimd(2, "b_words_second")
                product_on_scalar(0, 3)
                add_on_gpsimd(3)
                multiply_base(4)
                drain_base(4)
                product_on_scalar(0, 4)
                add_on_gpsimd(4)
            if m == 3:
                multiply_base(5)
                drain_base(5)
            if m == 1:
                multiply_base(2)
            if m + 2 < NB:
                interleave_helper(m + 2, 1)
                interleave_scalar(m + 2, 0)
                if m == 1:
                    drain_base(0)
                    drain_base(1)
                interleave_scalar(m + 2, 1)
            drain_h(m, 2)
            drain_h(m, 3)

        for_vector = [
            (m, j + k) for j in range(0, NJ, 2) for m in range(NB) for k in range(2) if j < FIRST_SHARED or m >= 2
        ]
        for_scalar = [(1, 2), (1, 3), (0, 5), (1, 4), (1, 5), (None, 6), (None, 7), (0, 6), (1, 6), (0, 7), (1, 7)]
        for k in range(VECTOR_BANKS):
            vector_ring.append(free_banks.pop(0))
        for pos, (m, j) in enumerate(for_vector):
            product_on_vector(m, j)
            if pos == 0:
                nc.vector.quantize_mx(
                    out=hl_late[1][:].rearrange("p k n -> p (k n)").bitcast(FP8X4),
                    scales=hl_late[2][:].rearrange("p k n -> p (k n)"),
                    in_=hl_late[0][:].rearrange("p k n t -> p (k n t)"),
                )
            if pos < len(for_scalar):
                late_m, late_j = for_scalar[pos]
                if late_m is None:
                    multiply_base(late_j)
                    drain_base(late_j)
                else:
                    product_on_scalar(late_m, late_j)
                    if late_j < FIRST_TWO_PARTS or late_m == 1:
                        add_on_gpsimd(late_j, "hl3" if pos == 0 else None)
            done_m, done_j = for_vector[max(pos - AHEAD, 0)]
            if done_m == NB - 1 and done_j % 2 == 1:
                first = done_j - 1
                for k in (first, first + 1):
                    nc.scalar.copy(out=out32_of(k, k + 1), in_=turn_result(k)[:])
                store_result(first, first + 2)
                dst, src = rounding_views(out32_of(first, first + 2), first, first + 2)
                if first < 4:
                    nc.gpsimd.tensor_scalar(out=dst, in0=src, scalar1=1.0, scalar2=-0.0, op0=MULT, op1=ADD)
                else:
                    nc.scalar.copy(out=dst, in_=src)

        free_banks.extend(vector_ring)
        for j in (NJ - 2, NJ - 1):
            turn_parts(j, parts[j][1:], True, False)
        for j in (NJ - 2, NJ - 1):
            bank = turn_result(j)
            dst, src = rounding_views(bank[:], j, j + 1)
            nc.vector.tensor_copy(out=dst, in_=src)
            nc.scalar.copy(out=out32_of(j, j + 1), in_=bank[:])
            store_result(j, j + 1)
        for g in range(2):
            turn_plane(g, 0, nc.vector.tensor_copy)
            turn_plane(g, 1, nc.scalar.copy)
        quantise_plane(0, 0)
        quantise_plane(0, 1)
        store_codes(0, 0, 2)
        for h in range(2):
            quantise_plane(1, h)
            store_codes(1, h, h + 1)
        for q in range(4):
            nc.scalar.dma_start(
                out=out_2[:, 4 * q : 4 * q + 4, :].bitcast(I32), in_=p_plane[32 * q : 32 * q + 8, :].bitcast(I32)
            )
